import numpy as np, ml_dtypes
CORES = [40,41,42,43,44,45,46,47]
N = 8
import mx_ref
BF = ml_dtypes.bfloat16
def gcols(t, e):
    v = np.concatenate([t.reshape(8, 16, -1, 4), np.zeros((8, 16, 1, 4), BF)], axis=2)
    return np.ascontiguousarray(np.stack([v[g][:, e[g]] for g in range(8)])).reshape(128, -1)
def tile(rs):
    return np.stack(rs, axis=2).reshape(128, -1).astype(BF)
def pick(q, e):
    c = np.concatenate([q[0].reshape(128, -1, 4), np.zeros((128, 1, 4), np.uint8)], axis=1); s = np.concatenate([q[1], np.ones((16, 1), np.uint8)], axis=1)
    return (np.ascontiguousarray(c[:, e].reshape(128, -1)), np.ascontiguousarray(s[:, e]))
def join(*qs):
    return (np.concatenate([q[0] for q in qs], axis=1), np.concatenate([q[1] for q in qs], axis=1))
def put(q, e, v):
    c, s = q[0].reshape(128, -1, 4).copy(), q[1].copy(); c[:, e] = v[0].reshape(128, -1, 4); s[:, e] = v[1]
    return (c.reshape(128, -1), s)
def pk(c, s):
    return (np.ascontiguousarray(c), mx_ref.live(s))
def emit(q):
    return q[0], q[1]
def packed(v, rng):
    q = [mx_ref.quantize(np.ascontiguousarray(v[r])) for r in range(N)]
    return np.stack([a for a, b in q]), np.stack([mx_ref.plane(b, rng) for a, b in q])
def values_of_codes():
    e, c = np.zeros((128, 128, 4), np.float32), np.zeros((128, 2, 4), np.uint8)
    e[np.arange(128), np.arange(128), 0] = 1
    c[:127, :, 0] = np.arange(256).reshape(2, 128).T[:127]
    return mx_ref.matmul(mx_ref.quantize(e.reshape(128, 512).astype(BF)), (c.reshape(128, 8), np.full((16, 2), 127, np.uint8))).T.reshape(-1).astype(np.float64)
CODE_VALUE, SCALE_VALUE = values_of_codes(), 2.0 ** (np.arange(256) - 127.0)
def decode(q):
    return (CODE_VALUE[q[0]].reshape(16, 8, -1, 4) * SCALE_VALUE[q[1]][:, None, :, None] + 0.0).reshape(128, -1).astype(np.float32)
def f(rng, *shape):
    return mx_ref.flush((rng.standard_normal(shape, dtype=np.float32) * np.exp2(rng.integers(-2, 3, shape[:-1] + (1,)))).astype(BF))
def wide(rng, *shape, cols=0):
    v = rng.standard_normal(shape, dtype=np.float32) * np.exp2(rng.integers(-12, 13, shape)).astype(np.float32)
    if cols: v *= np.repeat(np.exp2(rng.integers(-cols, cols + 1, shape[:-2] + (1, shape[-1] // 4))) * (rng.random(shape[:-2] + (1, shape[-1] // 4)) > 0.0625), 4, axis=-1).astype(np.float32)
    return mx_ref.flush(v.astype(BF))
C, A, B, S = 512, 256, 128, 16
def top(s, k):
    return np.sort(np.argsort(-s, axis=-1, kind="stable")[..., :k], axis=-1)
def layer(w, q):
    return tile([np.maximum(mx_ref.matmul(pick(w, np.arange(128 * b, 128 * b + 128)), q), np.float32(0.0)) * np.float32(0.03125) for b in range(4)])
def gadd(t, e, v):
    a, c = t.astype(np.float32).reshape(8, 16, -1, 4), v.astype(np.float32).reshape(8, 16, -1, 4)
    for g in range(8): a[g][:, e[g]] = a[g][:, e[g]] + c[g]
    return a.reshape(128, -1).astype(BF)
def big(v, k):
    v = v.astype(np.float32) * np.float32(k)
    v[np.abs(v) < np.float32(2.0 ** -16)] = 0
    return v.astype(BF)
def numbers_of(rng):
    return {"x": big(f(rng, N, 128, 4 * C), 1), "u1": np.array(f(rng, N, 128, 512)), "u2": np.array(f(rng, N, 128, 512)), "v": np.array(f(rng, N, 128, 512))}
def weights(rng, w, z):
    a, b = packed(w, rng)
    c, e = packed(z, rng)
    return {"wc": a, "ws": b, "zc": c, "zs": e}
def unit(k):
    w = np.zeros((N, 128, 4, 128, 4), np.float32)
    i = np.arange(128)
    for b in range(4): w[:, i, b, i, b] = k
    return w.reshape(N, 128, 2048).astype(BF)
def signs(rng):
    return np.stack([rng.permutation(8) % 2 * 2.0 - 1.0 for r in range(N)])
def steps(n):
    return np.minimum((np.arange(n) + 1) // 2, n // 2 - 1)
def planted(rng, p1, p2, k):
    d = numbers_of(rng)
    s1, t, s2 = np.zeros((N, 8, C), int), np.zeros((N, 8, A), int), np.zeros((N, 8, C), int)
    np.put_along_axis(s1, p1, np.broadcast_to(steps(C), p1.shape), axis=2)
    np.put_along_axis(t, p2, np.broadcast_to(steps(A), p2.shape), axis=2)
    first = top(s1, A)
    np.put_along_axis(s2, first, t, axis=2)
    x = d["x"].astype(np.float32).reshape(N, 8, 16, C, 4)
    x[:, :, 0] = 0
    x[:, :, 0, :, 0] = 1
    np.put_along_axis(x[:, :, 0, :, 1], p1[..., -1:], np.float32(2.0 ** 13), axis=2)
    np.put_along_axis(x[:, :, 0, :, 1], p1[..., :1], np.float32(-2.0 ** 30), axis=2)
    np.put_along_axis(x[:, :, 0, :, 2], np.take_along_axis(first, p2[..., -1:], axis=2), np.float32(2.0 ** 13), axis=2)
    for s, at in ((s1, 8), (s2, 10)):
        g = ((s[..., None] >> np.arange(8)) & 1) * np.exp2(np.arange(8) - 23.0)
        x[:, :, at] = g[..., :4]
        x[:, :, at + 1] = g[..., 4:]
    x[:, :, 12] = 0
    x[:, :, 12, :, 0] = 2.0 ** -10
    x[:, :, 13:] = rng.integers(4, 8, (N, 8, 3, C, 4)) * rng.choice([-1.0, 1.0], (N, 8, 3, C, 4)) * 2.0 ** -20
    d["x"] = x.reshape(N, 128, 4 * C).astype(BF)
    for n, at, far in (("u1", 8, 1), ("u2", 10, 2)):
        u = d[n].reshape(N, 128, 128, 4)
        u[:, :, ::16] = 0
        g = (signs(rng) * k).astype(BF)
        for i in range(8):
            u[:, 16 * i, 16 * i, 0] = g[:, i]
            u[:, 16 * i, 16 * i, far] = 2.0 ** 13 * k
            u[:, 16 * i + at:16 * i + at + 2, 16 * i] = k
            u[:, 16 * i + 12, 16 * i, 0] = g[:, i]
        d[n] = u.reshape(N, 128, 512)
    return {**d, **weights(rng, unit(32), f(rng, N, 128, 2048))}
def setup_inputs(rng):
    return {**numbers_of(rng), **weights(rng, f(rng, N, 128, 2048), f(rng, N, 128, 2048))}
def setup_inputs_ties(rng):
    d = numbers_of(rng)
    e = rng.permutation(N)
    x = d["x"].reshape(N, 8, 16, C, 4)
    for r in range(N):
        k = np.zeros(C, int) if r == e[0] else rng.permutation(C) % 3
        a = x[r][:, :8, :3].copy()
        a[:, :, 2] = 0
        x[r][:, :8] = a[:, :, k]
    d["x"] = x.reshape(N, 128, 4 * C)
    w = np.array(f(rng, N, 128, 2048)).reshape(N, 8, 16, 4, 8, 16, 4)
    w[:, :, 8:, :, :, :8] = 0
    for g in range(8): w[:, np.arange(8) != g, :, :, g, :8] = 0
    for n in ("u1", "u2"):
        u = d[n].reshape(N, 8, 16, 128, 4)
        u[:, :, 8:, ::16] = 0
        for g in range(8): u[:, np.arange(8) != g, :, 16 * g] = 0
        d[n] = u.reshape(N, 128, 512)
    return {**d, **weights(rng, w.reshape(N, 128, 2048), f(rng, N, 128, 2048))}
def setup_inputs_near(rng):
    p = []
    for n, k in ((C, A), (A, B)):
        a = rng.permuted(np.tile(np.arange(n), (N, 8, 1)), axis=2)
        a[:, :, n - k - 3:n - k + 1] = np.sort(a[:, :, n - k - 3:n - k + 1], axis=2)
        p.append(a)
    return planted(rng, p[0], p[1], 1.0)
def setup_inputs_runs(rng):
    a, b = signs(rng)[:, :, None] > 0, signs(rng)[:, :, None] > 0
    return planted(rng, np.where(a, np.arange(C), np.arange(C)[::-1]), np.where(b, np.arange(A), np.arange(A)[::-1]), 2.0 ** -30)
def setup_inputs_huge(rng):
    d = numbers_of(rng)
    c = np.stack([rng.permutation(C) % 2 * 2.0 - 1.0 for r in range(N)])
    c[rng.permutation(N) < N // 2] = -1
    x = 2.0 ** 30 * (0.6 + 0.3 * rng.random((N, 128, C, 4))) * c[:, None, :, None]
    d["x"] = x.astype(np.float32).reshape(N, 128, 4 * C).astype(BF)
    for n in ("u1", "u2"):
        u = d[n].reshape(N, 128, 128, 4)
        a = 2.0 ** 30 * (1 - 0.25 * rng.random((N, 128, 8, 4))) * signs(rng)[:, None, :, None]
        u[:, :, ::16] = a.astype(np.float32).astype(BF)
        d[n] = u.reshape(N, 128, 512)
    return {**d, **weights(rng, unit(-32), big(f(rng, N, 128, 2048), 2.0 ** -6))}
def setup_inputs_spread(rng):
    d = setup_inputs(rng)
    d["x"] = big(wide(rng, N, 128, 4 * C, cols=6), 1)
    return d
def check_inputs(d):
    b = []
    for k in ("x", "u1", "u2", "v"):
        a = np.abs(d[k].astype(np.float32))
        if not (np.isfinite(a).all() and ((a == 0) | (a >= 2.0 ** -30) & (a <= 2.0 ** 30)).all()): b.append("a value of " + k)
    return b
def reference(x, u1, u2, v, wc, ws, zc, zs):
    one, two, h, down = [], [], [], []
    for r in range(N):
        p = mx_ref.matmul(mx_ref.quantize(u1[r]), mx_ref.quantize(x[r]))
        one.append(top(p[::16] + np.float32(0.0), A))
        h.append(layer(pk(wc[r], ws[r]), mx_ref.quantize(gcols(x[r], one[r]))))
        p = mx_ref.matmul(mx_ref.quantize(u2[r]), mx_ref.quantize(h[r]))
        two.append(top(p[::16] + np.float32(0.0), B))
        down.append(mx_ref.quantize(gcols(h[r], two[r])))
    done = []
    for d in range(N):
        q = join(*[pick(down[r], S * d + np.arange(S)) for r in range(N)])
        done.append(mx_ref.quantize(layer(pk(zc[d], zs[d]), q)))
    y, ol = np.zeros((N, 128, C), np.float32), np.zeros((N, 8, B), np.float32)
    oc, osc = np.zeros((N, 128, 4 * C), np.uint8), np.zeros((N, 16, C), np.uint8)
    for r in range(N):
        came = decode(join(*[pick(done[d], S * r + np.arange(S)) for d in range(N)]))
        q = mx_ref.quantize(gadd(x[r], one[r], gadd(h[r], two[r], came)))
        y[r] = mx_ref.matmul(mx_ref.quantize(v[r]), q)
        ol[r] = np.take_along_axis(one[r], two[r], axis=1)
        oc[r], osc[r] = emit(q)
    return {"y": y, "ol": ol, "oc": oc, "osc": osc}

@@ -1,0 +1,459 @@
+from concourse.bass import DstId, RemoteDMATransfer
+from concourse.mybir import dt, AluOpType as A, AxisListType, ActivationFunctionType as AF
+
+F8, U8, BF, F32, I32, U16 = "float8_e4m3fn_x4", "uint8", "bfloat16", "float32", "int32", "uint16"
+SCRATCH = {}
+for _d, _l in (
+    (BF, "tu1 512 tu2 512 tv 512 tx 2048 xf 2048 tf 1024 th 1024 txh 1024 tg 512 tt 512 thn 512 txg 512 txn 512 ones 512 te 2048 "
+         "tot 528 jr 528 pre 528 val1 512 val2 256 sj 512 sjv 512 R1 1568 R2 800 Tr1 512 Tr2 256 Tr3 256 gap3 256 W1 16 W2 8 W3 8"),
+    (F32, "br 296 wt 296 iw 296 nt1 296 tbr 576 tbt 576 tb 24 seq 24 ft 16 ir 512 kr1 32 kr2 16 tr1 32 tr2 16 zero 32 c 64 gj 32 l64 96 "
+          "sc8 8 si8 8 sm 64 srow 512 ch1 32 ch2 16 gt 32 eq 32 gs 36 es 36 gsg 36 me 36 pi 36 kp 32 dd 32 mm 32 L1r 256 olr 128 ysb 512"),
+    (I32, "ip 8 ipick 8 itb 34 vi 32 vq 32 vg 32"),
+    (U16, "opick 8 otb 36 off 2 offb 2 offn 2 og 2 oe 2 osc1 32 osc2 16 o1 80 o2 40 o3 32")):
+    _l = _l.split()
+    for _i in range(0, len(_l), 2):
+        SCRATCH[_l[_i]] = ("sbuf", [128, int(_l[_i + 1])], _d)
+for _n, _w in (("W", 512), ("Z", 512), ("x", 512), ("N", 512), ("E", 512), ("F", 256), ("H", 256), ("u1", 128), ("u2", 128), ("r1", 128), ("r2", 128), ("v", 128),
+               ("G", 128), ("L", 128), ("T", 128), ("U", 128)):
+    SCRATCH["q" + _n] = ("sbuf", [128, _w], F8)
+    SCRATCH["s" + _n] = ("sbuf", [128, _w], U8)
+for _i in range(8):
+    SCRATCH["p%d" % _i] = ("psum", [128, 512], F32)
+SEMAPHORES = ["qv", "qa", "qt", "qg", "down", "up", "sent"] + ["d%d" % i for i in range(40)]
+
+
+def rank_program(g, core, T, topo):
+    rank = T.rank_of(core)
+    if rank is None:
+        return
+    N = len(T.cores)
+    V, S, P = g.vector, g.scalar, g.tensor
+    ENG = {"v": V, "a": S, "t": P, "g": g, "s": g.sync}
+    clock = {q: {} for q in ENG}
+    total, seen, wr, rd, nd = {}, {}, {}, {}, [0]
+
+    def learn(q, deps):
+        want = {}
+        for _, s, n, _c in deps:
+            want[s] = max(want.get(s, 0), n)
+        for s in sorted(want):
+            n = want[s]
+            if clock[q].get(s, 0) >= n:
+                continue
+            if any(d[1] != s and want[d[1]] == d[2] and d[3].get(s, 0) >= n for d in deps if clock[q].get(d[1], 0) < d[2]):
+                continue
+            ENG[q].wait_ge(T.sem[s], n)
+            seen[s] = max(seen.get(s, 0), n)
+        for d in deps:
+            for s, n in list(d[3].items()) + [(d[1], d[2])]:
+                clock[q][s] = max(clock[q].get(s, 0), n)
+
+    def deps_of(r, w):
+        deps = []
+        for t in r:
+            deps += wr.get(t, [])
+        for t in w:
+            deps += wr.get(t, []) + rd.get(t, [])
+        return deps
+
+    def note(q, s, n, r, w, base):
+        e = (q, s, n, dict(base))
+        for t in w:
+            wr[t], rd[t] = [e], []
+        for t in r:
+            if t not in w:
+                rd.setdefault(t, []).append(e)
+
+    def do(q, fn, *a, r=(), w=(), **k):
+        learn(q, deps_of(r, w))
+        s = "q" + q
+        total[s] = total.get(s, 0) + 1
+        fn(*a, **k).then_inc(T.sem[s], 1)
+        note(q, s, total[s], r, w, clock[q])
+
+    def dma(q, out, in_, r=(), w=(), **k):
+        learn(q, deps_of(r, w))
+        s = "d%d" % nd[0]
+        nd[0] += 1
+        total[s] = 16
+        ENG[q].dma_start(out, in_, **k).then_inc(T.sem[s], 16)
+        note(q, s, 16, r, w, clock[q])
+
+    def mm(p, n, a, ac, b, bc, r):
+        do("t", P.matmul_mx, T[p][:, 0:n], T["q" + a][:, ac:ac + 128], T["s" + a][:, ac:ac + 128], T["q" + b][:, bc:bc + n], T["s" + b][:, bc:bc + n], True, True, r=r, w=[p])
+
+    def quant(q, c, n, t, r, w, tc=None):
+        tc = 4 * c if tc is None else tc
+        do("v", V.quantize_mx, T["q" + q][:, c:c + n], T["s" + q][:, c:c + n], t[:, tc:tc + 4 * n], r=r, w=[w])
+
+    def ts(out, in0, s1, op0, r, w, s2=None, op1=None):
+        do("v", V.tensor_scalar, out, in0, s1, s2, op0, *([] if op1 is None else [op1]), r=r, w=[w])
+
+    def tt(out, a, b, op, r, w):
+        do("v", V.tensor_tensor, out, a, b, op, r=r, w=[w])
+
+    def red(out, in_, op, r, w):
+        do("v", V.tensor_reduce, out, in_, AxisListType.X, op, r=r, w=[w])
+
+    def fill(ap, x, w):
+        do("v", V.memset, ap, x, w=[w])
+
+    def cp(out, in_, r, w):
+        do("v", V.tensor_copy, out, in_, r=r, w=[w])
+
+    def act(out, in_, f, r, w, **k):
+        do("a", S.activation, out, in_, f, r=r, w=w, **k)
+
+    def codes(v):
+        return v.bitcast(dt.uint8)
+
+    def words(v):
+        return v.bitcast(dt.uint32)
+
+    def cc(j):
+        return T.c[:, j:j + 1]
+
+    def sm(j):
+        return T.sm[:, j:j + 1]
+
+    dma("s", T.tu1[:, :], T.u1[:, :], w=["tu1"])
+    for j in range(4):
+        dma("a" if j % 2 == 0 else "s", T.tx[:, 512 * j:512 * j + 512], T.x[:, 512 * j:512 * j + 512], w=["tx%d" % j])
+    X = ["tx%d" % j for j in range(4)]
+
+    def iota(n, pattern, base, cm=0):
+        k = 1
+        for _s, m in pattern:
+            k *= m
+        f = {} if SCRATCH[n][2] == I32 else {"allow_small_or_imprecise_dtypes": True}
+        do("g", g.iota, T[n][:, 0:k], pattern, base, cm, w=[n], **f)
+    iota("ip", [[1, 1]], 0, 1)
+    iota("itb", [[17, 17], [0, 2]], 1)
+    iota("ipick", [[16, 8]], 0)
+    iota("seq", [[17, 17]], 0)
+    iota("tot", [[0, 16], [1, 33]], 0)
+    iota("jr", [[1, 16], [0, 33]], 0)
+    iota("kr1", [[1, 32]], 256)
+    iota("kr2", [[1, 16]], 128)
+    iota("val1", [[1, 32], [32, 16]], -256)
+    iota("val2", [[1, 16], [16, 16]], 0)
+    iota("ir", [[1, 512]], 0)
+    LANE, ODD, LP1, CN, CP, L33, O16, EVEN, L32, M8, E8, D6, L16, EB = range(14)
+    ts(T.ip[:, 1:2], T.ip[:, 0:1], 15, A.bitwise_and, ["ip"], "ip1")
+    ts(T.ip[:, 2:3], T.ip[:, 0:1], 4, A.logical_shift_right, ["ip"], "ip2", 1, A.bitwise_and)
+    cp(cc(LANE), T.ip[:, 1:2], ["ip1"], "lane")
+    cp(cc(ODD), T.ip[:, 2:3], ["ip2"], "odd")
+    fill(T.br[:, 146:147], 2.0 ** -70, "br2")
+    fill(T.br[:, 0:1], -2.0 ** 75, "br")
+    ts(cc(CN), cc(LANE), 0.0625, A.mult, ["lane"], "cn", -1.9375, A.add)
+    ts(cc(CP), cc(LANE), -0.0625, A.mult, ["lane"], "cp", -1.0625, A.add)
+    k = 1
+    while k < 146:
+        s = min(k, 64)
+        n1, n2 = min(2 * k, 146) - k, min(2 * k, 144) - k
+        ts(T.br[:, k:k + n1], T.br[:, k - s:k - s + n1], 2.0 ** -s, A.mult, ["br"], "br")
+        if n2 > 0:
+            act(T.br[:, 146 + k:146 + k + n2], T.br[:, 146 + k - s:146 + k - s + n2], AF.Identity, ["br2"], ["br2"], scale=2.0 ** s)
+        k *= 2
+    B = ["br", "br2"]
+    act(T.nt1[:, 0:145], T.br[:, 1:146], AF.Identity, ["br", "cn"], ["nta"], scale=cc(CN))
+    act(T.nt1[:, 146:289], T.br[:, 146:289], AF.Identity, ["br2", "cp"], ["ntb"], scale=cc(CP))
+    act(T.wt[:, 0:145], T.br[:, 1:146], AF.Identity, ["br"], ["wta"], scale=-1.0)
+    act(T.wt[:, 146:289], T.br[:, 146:289], AF.Identity, ["br2"], ["wtb"])
+    act(T.iw[:, 4:145], T.br[:, 146:287], AF.Identity, ["br2"], ["iwa"])
+    act(T.iw[:, 146:287], T.br[:, 5:146], AF.Identity, ["br"], ["iwb"], scale=-1.0)
+    NT, WT, IW = ["nta", "ntb", "ntc", "ntd"], ["wta", "wtb", "wtc", "wtd"], ["iwa", "iwb", "iwc", "iwd", "iwe"]
+    for r in range(6):
+        act(cc(40 + r), T.br[:, 146:147], AF.Identity, ["br2"], ["crow%d" % r], scale=[-2.0 ** 66, -2.0 ** 62, -2.0 ** 58, -2.0 ** 54, 2.0 ** 50, 2.0 ** 47][r])
+        act(cc(48 + r), T.br[:, 146:147], AF.Identity, ["br2"], ["drow%d" % r], scale=[-2.0 ** 74, -2.0 ** 78, -2.0 ** 82, -2.0 ** 86, -2.0 ** 90, 2.0 ** 93][r])
+
+    def lin(j, w, src, k, add):
+        act(cc(j), cc(src), AF.Identity, ["lane", "odd"], [w], scale=k, bias=add)
+
+    def const(b, c, n, x, w):
+        act(T[b][:, c:c + n], T.br[:, 0:n], AF.Identity, ["br"], [w], scale=0.0, bias=x)
+    lin(56, "cb", LANE, -0.9375, -0.9375)
+    lin(E8, "e8", LANE, 0.125, -3.875)
+    const("iw", 0, 4, 1.0, "iwc")
+    const("iw", 145, 1, 2.0 ** 69, "iwd")
+    const("iw", 287, 9, 1.0, "iwe")
+    const("wt", 145, 1, 2.0 ** -69, "wtc")
+    const("wt", 289, 7, 1.0, "wtd")
+    const("nt1", 289, 7, 1.0, "ntd")
+    act(T.nt1[:, 145:146], cc(LANE), AF.Identity, ["lane"], ["ntc"], scale=-(2.0 ** -73), bias=7 * 2.0 ** -73)
+    lin(L33, "l33", LANE, 33.0, 0.0)
+    lin(O16, "o16", ODD, 16.0, 0.0)
+    lin(L32, "l32", LANE, 32.0, 0.0)
+    ts(T.otb[:, 0:34], T.itb[:, :], cc(LANE), A.add, ["itb", "lane"], "otba")
+    ts(T.otb[:, 34:35], cc(LANE), 17.0, A.mult, ["lane"], "otbb", 17.0, A.add)
+    ts(T.otb[:, 35:36], cc(LANE), 17.0, A.mult, ["lane"], "otbc", 17.0, A.add)
+    cp(T.opick[:, :], T.ipick[:, :], ["ipick"], "opick")
+    ts(T.off[:, 1:2], cc(LANE), 0.0, A.is_equal, ["lane"], "off1", 8.0, A.mult)
+    ts(cc(LP1), cc(LANE), 1.0, A.add, ["lane"], "lp1")
+    cp(T.tbr[:, :], T.br[:, 0:290].indirect(T.otb[:, :]), B + ["otba", "otbb", "otbc"], "tbr")
+    do("v", V.transpose, T.tbt[:, :], T.tbr[:, :], r=["tbr"], w=["tbt"])
+    ts(T.tb[:, 0:18], T.tbt[:, 0:576:32], -1.0, A.mult, ["tbt"], "tb")
+    quant("u1", 0, 128, T.tu1, ["tu1"], "qu1")
+    cp(words(T.qr1[:, :]), words(T.qu1[:, :]).indirect(T.opick[:, :]), ["qu1", "opick"], "qr1")
+    act(T.sr1[:, :], T.su1[:, :].indirect(T.opick[:, :]), AF.Copy, ["qu1", "opick"], ["sr1"])
+    fill(T.ft[:, 0:16], 0.0, "base")
+    do("v", V.memset, T.ft[:, 1:2], 1.0, r=["base"], w=["fta"])
+    FT = ["fta", "base"]
+
+    for j in range(4):
+        quant("x", 128 * j, 128, T.tx, ["tx%d" % j], "qx%d" % j)
+    R = ["qr1", "sr1"]
+    mm("p2", 384, "r1", 0, "x", 0, ["qx0", "qx1", "qx2"] + R)
+    mm("p3", 128, "r1", 0, "x", 384, ["qx3"] + R)
+    for p in ("p0", "p1"):
+        mm(p, 512, "r1", 0, "x", 0, ["qx%d" % j for j in range(4)] + R)
+
+    learn("s", [d for t in X for d in wr[t]])
+    dma("s", T.tu2[:, :], T.u2[:, :], w=["tu2"])
+    dma("s", codes(T.qW[:, :]), T.wc[:, :], w=["qW"])
+    dma("s", T.sW[:, :], T.ws[:, :], w=["sW"])
+
+    def jobs1():
+        ts(cc(M8), cc(LANE), 8.0, A.is_lt, ["lane"], "m8")
+        ts(cc(D6), cc(E8), cc(M8), A.mult, ["e8", "m8"], "d6", 4.0, A.add)
+        ts(cc(60), cc(D6), cc(LP1), A.subtract, ["d6", "lp1"], "cb5")
+        ts(cc(61), cc(D6), -8.0, A.mult, ["d6"], "cb6")
+        fill(T.zero[:, :], 0.0, "zero")
+        fill(T.gs[:, 0:1], 0.0, "gs0")
+        fill(T.es[:, 0:1], 0.0, "es0")
+        yield
+        ts(T.pre[:, :], T.jr[:, :], cc(LANE), A.is_lt, ["jr", "lane"], "prea")
+        ts(T.tr1[:, :], T.kr1[:, :], cc(L32), A.add, ["kr1", "l32"], "tr1")
+        yield
+        tt(T.pre[:, 0:264], T.pre[:, 0:264], T.tot[:, 0:264], A.mult, ["prea", "tot"], "preb")
+        yield
+        tt(T.pre[:, 264:528], T.pre[:, 264:528], T.tot[:, 264:528], A.mult, ["prea", "tot"], "prec")
+        yield
+        fill(T.R1[:, 0:512], 0.0, "R1")
+        quant("u2", 0, 128, T.tu2, ["tu2"], "qu2")
+        yield
+
+    def jobs2():
+        fill(T.ones[:, :], 1.0, "ones")
+        for b in range(4):
+            do("g", g.affine_select, T.te[:, 512 * b:512 * b + 512], T.ones[:, :], [[1, 512]], A.is_equal, 0.0, -b, -4, r=["ones"], w=["te%d" % b])
+        ts(cc(L16), cc(LANE), 16.0, A.mult, ["lane"], "l16")
+        yield
+        fill(T.R2[:, 0:256], 0.0, "R2")
+        ts(T.tr2[:, :], T.kr2[:, :], cc(L16), A.add, ["kr2", "l16"], "tr2")
+        ts(cc(EVEN), cc(ODD), -1.0, A.mult, ["odd"], "even", 1.0, A.add)
+        ts(cc(EB), cc(EVEN), -256.0, A.mult, ["even"], "eb")
+        yield
+
+    def search(n, pa, pb, first, ch, jobs):
+        q = n // 16
+
+        def job():
+            for _ in jobs:
+                return
+
+        def count(bias, j, r, p=pa, w=n):
+            act(T.sj[:, 0:w], T[p][:, 0:w], AF.Sign, [p, r], ["sj", "sm%d" % j], bias=bias, accum_out=sm(j))
+
+        def answer(j):
+            ts(T.off[:, 0:1], sm(j), 0.0, A.is_ge, ["sm%d" % j], "off0")
+        for j, (p, w) in enumerate(first):
+            count(T.tb[:, 17:18], j, "tb", p, w)
+        job()
+        if len(first) == 2:
+            ts(sm(1), sm(0), sm(1), A.add, ["sm0", "sm1"], "sm2", 0.0, A.is_ge)
+            ts(T.offb[:, 0:1], sm(1), cc(LP1), A.mult, ["sm2", "lp1"], "offb")
+        else:
+            ts(T.offb[:, 0:1], sm(0), 0.0, A.is_ge, ["sm0", "lp1"], "offb", cc(LP1), A.mult)
+        cp(T.l64[:, 0:16], T.tb[:, 0:17].indirect(T.offb[:, 0:1]), ["offb", "tb"], "b16")
+        red(sm(3), T.l64[:, 0:16], A.min, ["b16"], "sm3")
+        count(sm(3), 4, "sm3")
+        cp(T.l64[:, 64:80], T.seq[:, 0:17].indirect(T.offb[:, 0:1]), ["offb", "seq"], "s16")
+        red(sm(5), T.l64[:, 64:80], A.max, ["s16"], "sm5")
+        job()
+        answer(4)
+        act(T.gj[:, 0:16], T.ft[:, 0:8].indirect(T.off[:, 0:1]), AF.Identity, ["off0"] + FT, ["gj", "sm6"], accum_out=sm(6))
+        ts(T.offn[:, 0:1], sm(6), sm(5), A.add, ["sm6", "sm5"], "offn")
+        act(T.l64[:, 16:32], T.nt1[:, 0:296].indirect(T.offn[:, 0:1]), AF.Identity, ["offn"] + NT, ["n16"])
+        cp(T.l64[:, 32:48], T.iw[:, 0:296].indirect(T.offn[:, 0:1]), ["offn"] + IW, "i16")
+        cp(T.l64[:, 48:64], T.wt[:, 0:296].indirect(T.offn[:, 0:1]), ["offn"] + WT, "w16")
+        ts(T.si8[:, 0:6], T.c[:, 48:54], T.l64[:, 32:33], A.mult, ["i16"] + ["drow%d" % j for j in range(6)], "si8")
+        ts(T.sc8[:, 0:6], T.c[:, 40:46], T.l64[:, 48:49], A.mult, ["w16"] + ["crow%d" % j for j in range(6)], "sc8")
+        t, tk = T.l64[:, 16:17], "n16"
+        for r in range(6):
+            nx = "sm%d" % (16 + r)
+            cb = cc(56 if r < 4 else 56 + r)
+            cr = [tk, "si8", ["cb", "cb5", "cb6"][max(r - 3, 0)]]
+            if r < 5:
+                count(t, 8 + r, tk)
+                ts(T.ft[:, 8:9], t, T.si8[:, r:r + 1], A.mult, cr, "base", cb, A.add)
+                if r == 1:
+                    cp(T.srow[:, 0:n], T[pb][:, 0:n], [pb], "srow")
+                    dma("s", ch[:, :], T.srow[0:128:16, 0:n], r=["srow"], w=["ch"])
+                elif r > 1:
+                    job()
+                answer(8 + r)
+            else:
+                m = n // 2
+                ts(T.sjv[:, 0:m], T[pb][:, 0:m], t, A.is_ge, [pb, tk], "sjv0")
+                ts(T.sjv[:, m:n], T[pb][:, m:n], t, A.is_ge, [pb, tk], "sjv1")
+                act(T.sj[:, 0:m], T.sjv[:, 0:m], AF.Copy, ["sjv0"], ["sj", "sm13"], accum_out=sm(13))
+                red(sm(14), T.sjv[:, m:n], A.add, ["sjv1"], "sm14")
+                ts(T.ft[:, 8:9], t, T.si8[:, r:r + 1], A.mult, cr, "base", cb, A.add)
+                ts(T.off[:, 0:1], sm(14), sm(13), A.add, ["sm13", "sm14"], "off0", n / 2.0, A.is_ge)
+            act(T.gj[:, 0:32], T.ft[:, :].indirect(T.off[:, 0:2]), AF.Identity, ["off0", "off1", "sc8"] + FT, ["gj", nx], scale=T.sc8[:, r:r + 1], accum_out=sm(16 + r))
+            t, tk = sm(16 + r), nx
+        for _ in jobs:
+            pass
+        ts(T.gt[:, 0:q], ch[:, :], t, A.is_gt, ["ch", tk], "gt")
+        ts(T.eq[:, 0:q], ch[:, :], t, A.is_equal, ["ch", tk], "eq")
+        do("v", V.tensor_tensor_scan, T.gs[:, 1:q + 1], T.gt[:, 0:q], T.zero[:, 0:q], 0.0, A.add, A.add, r=["gt", "zero"], w=["gs"])
+        do("v", V.tensor_tensor_scan, T.es[:, 1:q + 1], T.eq[:, 0:q], T.zero[:, 0:q], 0.0, A.add, A.add, r=["eq", "zero"], w=["es"])
+        ts(T.og[:, 0:1], T.gs[:, q:q + 1], cc(L33), A.add, ["gs", "l33"], "og")
+        ts(T.oe[:, 0:1], T.es[:, q:q + 1], cc(L33), A.add, ["es", "l33"], "oe")
+        for tab, o, j in (("tot", "og", 31), ("pre", "og", 30), ("pre", "oe", 32)):
+            act(T.gj[:, 0:16], T[tab][:, :].indirect(T[o][:, 0:1]), AF.Identity, [o] + (["preb", "prec"] if tab == "pre" else ["tot"]), ["gj", "sm%d" % j], accum_out=sm(j))
+        tr, trk = (T.tr1, "tr1") if n == 512 else (T.tr2, "tr2")
+        ts(sm(33), sm(31), -1.0, A.mult, ["sm31"], "sm33", n / 2.0, A.add)
+        ts(T.gsg[:, 0:q + 1], T.gs[:, 0:q + 1], sm(30), A.add, ["gs0", "gs", "sm30"], "gsg")
+        ts(T.me[:, 0:q + 1], T.es[:, 0:q + 1], sm(32), A.add, ["es0", "es", "sm32", "sm33"], "me", sm(33), A.min)
+        tt(T.pi[:, 0:q + 1], T.gsg[:, 0:q + 1], T.me[:, 0:q + 1], A.add, ["gsg", "me"], "pi")
+        tt(T.kp[:, 0:q], T.pi[:, 1:q + 1], T.pi[:, 0:q], A.subtract, ["pi"], "kp")
+        tt(T.dd[:, 0:q], T.pi[:, 0:q], tr[:, :], A.subtract, ["pi", trk], "dd")
+        tt(T.mm[:, 0:q], T.dd[:, 0:q], T.kp[:, 0:q], A.mult, ["dd", "kp"], "mm")
+        tt(T.vi[:, 0:q], T.mm[:, 0:q], tr[:, :], A.add, ["mm", trk], "vi")
+        ts(T.vq[:, 0:q], T.vi[:, 0:q], 1008, A.bitwise_and, ["vi"], "vq")
+        tt(T.vg[:, 0:q], T.vi[:, 0:q], T.vq[:, 0:q], A.add, ["vi", "vq"], "vg")
+        so, R, rk, val, vk, Tr, W = (T.osc1, T.R1, "R1", T.val1, "val1", T.Tr1, T.W1) if n == 512 else (T.osc2, T.R2, "R2", T.val2, "val2", T.Tr2, T.W2)
+        ts(so[:, :], T.vg[:, 0:q], cc(O16), A.add, ["vg", "o16"], "so")
+        cp(R[:, :].indirect(so[:, :]), val[:, :], ["so", vk], rk)
+        do("v", V.transpose, Tr[:, :], R[:, 0:n], r=[rk], w=["Tr"])
+        tt(W[:, :], Tr[:, 0:n:32], Tr[:, 16:n:32], A.add, ["Tr"], "W%d" % n)
+
+    def offsets(o, w, W, k, add):
+        for t in range(4):
+            ts(T[o][:, k * t:k * t + k], W[:, :], 4.0, A.mult, [w], "%s_%d" % (o, t), add + t, A.add)
+
+    def gather(dst, m, src, rs, o, k, eng):
+        for t in range(4):
+            a = (T[dst][:, t:4 * m:4], src[:, :].indirect(T[o][:, k * t:k * t + k]))
+            r, w = rs + ["%s_%d" % (o, t)], "%s%d" % (dst, t)
+            if eng[t] == "a":
+                act(*a, AF.Copy, r, [w])
+            else:
+                cp(*a, r, w)
+
+    def layer(dst, q, b4, n, r):
+        for b in range(4):
+            p = "p%d" % (2 + b)
+            mm(p, n, q, 128 * b, b4, 0, r)
+            if b % 2 == 0:
+                act(T[dst][:, b:4 * n:4], T[p][:, 0:n], AF.Relu, [p], ["%s%d" % (dst, b)], scale=0.03125)
+            else:
+                ts(T[dst][:, b:4 * n:4], T[p][:, 0:n], 0.0, A.max, [p], "%s%d" % (dst, b), 0.03125, A.mult)
+
+    def four(n):
+        return ["%s%d" % (n, t) for t in range(4)]
+
+    search(512, "p0", "p1", [("p2", 384), ("p3", 128)], T.ch1, jobs1())
+    dma("s", codes(T.qZ[:, :]), T.zc[:, :], w=["qZ"])
+    dma("s", T.sZ[:, :], T.zs[:, :], w=["sZ"])
+    dma("s", T.tv[:, :], T.v[:, :], w=["tv"])
+    dma("s", T.xf[:, :], T.x[:, :], w=["xf"])
+    offsets("o1", "W512", T.W1, 16, 1024.0)
+    gather("tf", 256, T.tx, X, "o1", 16, "avav")
+    act(T.sr2[:, :], T.su2[:, :].indirect(T.opick[:, :]), AF.Copy, ["qu2", "opick"], ["sr2"])
+    quant("F", 0, 256, T.tf, four("tf"), "qF")
+    cp(words(T.qr2[:, :]), words(T.qu2[:, :]).indirect(T.opick[:, :]), ["qu2", "opick"], "qr2")
+    layer("th", "W", "F", 256, ["qW", "sW", "qF"])
+    dma("s", T.txh[:, :], T.tf[:, :], r=four("tf"), w=["txh"])
+    dma("g", T.txh[:, :], T.th[:, :], r=four("th"), w=["txh"], accum_op=A.add)
+    quant("H", 0, 256, T.th, four("th"), "qH")
+    for p in ("p6", "p7"):
+        mm(p, 256, "r2", 0, "H", 0, ["qH", "qr2", "sr2"])
+    search(256, "p6", "p7", [("p6", 256)], T.ch2, jobs2())
+    offsets("o2", "W256", T.W2, 8, 0.0)
+    gather("tg", 128, T.th, four("th"), "o2", 8, "avav")
+    quant("G", 0, 128, T.tg, four("tg"), "qG")
+
+    far = [d for d in range(N) if d != rank and topo.die(T.cores[d]) != topo.die(core)]
+    near = [d for d in range(N) if d != rank and topo.die(T.cores[d]) == topo.die(core)]
+    masks = {}
+    for lst, o in ((far, 0), (near, 1)):
+        for j, d in enumerate(lst):
+            e = topo.engines(core, T.cores[d])
+            masks[d] = sum(1 << x for x in (e[4 * j + o], e[4 * j + o + 2]))
+    order = sorted(masks, key=lambda d: (d - rank) % N)
+
+    def swap(a, b, sem):
+        own = slice(16 * rank, 16 * rank + 16)
+        tok = "q" + a
+        dma("s", codes(T["q" + b][:, own]), codes(T["q" + a][:, own]), r=[tok], w=[tok + "o"])
+        dma("s", T["s" + b][:, own], T["s" + a][:, own], r=[tok], w=[tok + "p"])
+        learn("g", wr[tok])
+        for x in "qs":
+            tr = []
+            for d in order:
+                rid, pid, _ = topo.addr(T.cores[d])
+                src, dst = T[x + a][:, 16 * d:16 * d + 16], T[x + b][:, own]
+                if x == "q":
+                    src, dst = codes(src), codes(dst)
+                tr.append(RemoteDMATransfer(dst_ids=[DstId(rid=rid, pnc=pid)], dma_engine_mask=masks[d], remote_sem=T.sem[sem], src=src, dst=dst))
+            g.remote_dma_fused(tr, local_sem=T.sem.sent)
+        total[sem] = 4 * (N - 1)
+        wr[tok + "r"] = [("far", sem, total[sem], {})]
+        total["sent"] = total.get("sent", 0) + 4 * (N - 1)
+    swap("G", "L", "down")
+    ts(T.o1[:, 64:80], T.W1[:, :], 256.0, A.add, ["W512"], "o1c")
+    cp(T.o2[:, 32:40], T.W2[:, :], ["W256"], "o2c")
+    act(T.L1r[:, :], T.ir[:, :].indirect(T.o1[:, 64:80]), AF.Identity, ["ir", "o1c"], ["L1r"])
+    act(T.olr[:, :], T.L1r[:, :].indirect(T.o2[:, 32:40]), AF.Identity, ["L1r", "o2c"], ["olr"])
+    dma("s", T.ol[:, :], T.olr[0:128:16, :], r=["olr"], w=["ol"])
+
+    def base(t):
+        cp(T.xf[:, :].indirect(T.o1[:, 16 * t:16 * t + 16]), T.txh[:, t:1024:4], ["o1_%d" % t, "txh"], "xf")
+    base(0)
+    for b in range(8):
+        i = T.olr[:, 16 * b:16 * b + 16]
+        act(T.gap3[:, 32 * b:32 * b + 16], i, AF.Identity, ["olr", "even", "eb"], ["gap%d" % b], scale=cc(EVEN), bias=cc(EB))
+        ts(T.gap3[:, 32 * b + 16:32 * b + 32], i, -256.0, A.add, ["olr", "odd"], "gap%d" % (8 + b), cc(ODD), A.mult)
+    do("v", V.transpose, T.Tr3[:, :], T.gap3[:, :], r=["gap%d" % b for b in range(16)], w=["Tr3"])
+    tt(T.W3[:, :], T.Tr3[:, 0:256:32], T.Tr3[:, 16:256:32], A.add, ["Tr3"], "W3")
+    offsets("o3", "W3", T.W3, 8, 1024.0)
+    base(1)
+    layer("tt", "Z", "L", 128, ["qZ", "sZ", "qGo", "qGp", "qGr"])
+    quant("T", 0, 128, T.tt, four("tt"), "qT")
+    swap("T", "U", "up")
+    for b in range(4):
+        quant("E", 128 * b, 128, T.te, ["te%d" % b], "qE%d" % b, 512 * b)
+    quant("v", 0, 128, T.tv, ["tv"], "qvv")
+    base(2)
+    base(3)
+    gather("txg", 128, T.tx, X, "o3", 8, "aaaa")
+    for b in range(4):
+        mm("p%d" % (2 + b), 128, "E", 128 * b, "U", 0, ["qE%d" % b, "qTo", "qTp", "qTr"])
+    for b in range(4):
+        tt(T.thn[:, b:512:4], T["p%d" % (2 + b)][:, 0:128], T.tg[:, b:512:4], A.add, ["p%d" % (2 + b), "tg%d" % b], "thn%d" % b)
+    for b in range(4):
+        tt(T.txn[:, b:512:4], T.txg[:, b:512:4], T.thn[:, b:512:4], A.add, ["txg%d" % b, "thn%d" % b], "txn%d" % b)
+    for b in range(4):
+        cp(T.xf[:, :].indirect(T.o3[:, 8 * b:8 * b + 8]), T.txn[:, b:512:4], ["o3_%d" % b, "txn%d" % b], "xf")
+    for h, (c, n) in enumerate(((0, 256), (256, 128), (384, 128))):
+        p = "p%d" % h
+        quant("N", c, n, T.xf, ["xf"], "qN%d" % h)
+        mm(p, n, "v", 0, "N", c, ["qvv", "qN%d" % h])
+    for h, (c, n) in enumerate(((0, 256), (256, 128), (384, 128))):
+        o, i = T.ysb[:, c:c + n], T["p%d" % h][:, 0:n]
+        if h < 2:
+            act(o, i, AF.Copy, ["p%d" % h], ["y%d" % h])
+        else:
+            cp(o, i, ["p%d" % h], "y%d" % h)
+    dma("s", T.oc[:, 0:1024], codes(T.qN[:, 0:256]), r=["qN0"], w=["oc0"])
+    dma("s", T.oc[:, 1024:2048], codes(T.qN[:, 256:512]), r=["qN1", "qN2"], w=["oc1"])
+    for j in range(4):
+        dma("s", T.osc[4 * j:4 * j + 4, :], T.sN[32 * j:32 * j + 4, :], r=["qN0", "qN1", "qN2"], w=["osc%d" % j])
+    dma("s", T.y[:, 0:256], T.ysb[:, 0:256], r=["y0"], w=["yo0"])
+    dma("a", T.y[:, 256:512], T.ysb[:, 256:512], r=["y1", "y2"], w=["yo1"])
+    for s in sorted(total):
+        if seen.get(s, 0) < total[s]:
+            g.wait_ge(T.sem[s], total[s])

@@ -5,11 +5,11 @@ F8, U8, BF, F32, I32, U16 = "float8_e4m3fn_x4", "uint8", "bfloat16", "float32", 
 SCRATCH = {}
 for _d, _l in (
     (BF, "tu1 512 tu2 512 tv 512 tx 2048 xf 2048 tf 1024 th 1024 txh 1024 tg 512 tt 512 thn 512 txg 512 txn 512 ones 512 te 2048 "
-         "tot 528 jr 528 pre 528 val1 512 val2 256 sj 512 sjv 512 R1 1568 R2 800 Tr1 512 Tr2 256 Tr3 256 gap3 256 W1 16 W2 8 W3 8"),
-    (F32, "br 296 wt 296 iw 296 nt1 296 tbr 576 tbt 576 tb 24 seq 24 ft 16 ir 512 kr1 32 kr2 16 tr1 32 tr2 16 zero 32 c 64 gj 32 l64 96 "
-          "sc8 8 si8 8 sm 64 srow 512 ch1 32 ch2 16 gt 32 eq 32 gs 36 es 36 gsg 36 me 36 pi 36 kp 32 dd 32 mm 32 L1r 256 olr 128 ysb 512"),
-    (I32, "ip 8 ipick 8 itb 34 vi 32 vq 32 vg 32"),
-    (U16, "opick 8 otb 36 off 2 offb 2 offn 2 og 2 oe 2 osc1 32 osc2 16 o1 80 o2 40 o3 32")):
+         "tot 528 jr 528 pre 528 val1 512 val2 256 sj 512 sjv 512 R1 1056 R2 544 Tr1 512 Tr2 256 Tr3 1024 gap3 1024 W1 16 W2 8 W3 96"),
+    (F32, "br 296 wt 296 iw 296 nt1 296 tbr 128 tbt 128 tb 24 seq 24 ft 16 ir 512 kr1 32 kr2 16 tr1 32 tr2 16 zero 32 c 64 gj 32 l64 96 "
+          "sc8 8 si8 8 sm 64 srow 512 ch1 32 ch2 16 gt 32 eq 32 gs 36 es 36 gsg 36 me 36 kp 32 dd 32 mm 32 vg 32 L1r 256 olr 128 ysb 512"),
+    (I32, "ip 8 ipick 8 itb 4 irep 64 vi 36 vq 32"),
+    (U16, "opick 8 otb 8 orep 64 off 2 offb 2 offn 2 og 2 oe 2 osc1 32 osc2 16 o1 80 o2 40 o3 32")):
     _l = _l.split()
     for _i in range(0, len(_l), 2):
         SCRATCH[_l[_i]] = ("sbuf", [128, int(_l[_i + 1])], _d)
@@ -128,25 +128,35 @@ def rank_program(g, core, T, topo):
         f = {} if SCRATCH[n][2] == I32 else {"allow_small_or_imprecise_dtypes": True}
         do("g", g.iota, T[n][:, 0:k], pattern, base, cm, w=[n], **f)
     iota("ip", [[1, 1]], 0, 1)
-    iota("itb", [[17, 17], [0, 2]], 1)
+    iota("itb", [[62, 2], [0, 2]], 75)
     iota("ipick", [[16, 8]], 0)
     iota("seq", [[17, 17]], 0)
     iota("tot", [[0, 16], [1, 33]], 0)
     iota("jr", [[1, 16], [0, 33]], 0)
-    iota("kr1", [[1, 32]], 256)
-    iota("kr2", [[1, 16]], 128)
+    iota("kr1", [[1, 32]], 512)
+    iota("kr2", [[1, 16]], 256)
     iota("val1", [[1, 32], [32, 16]], -256)
+    iota("irep", [[4, 32], [0, 2]], 0)
     iota("val2", [[1, 16], [16, 16]], 0)
     iota("ir", [[1, 512]], 0)
-    LANE, ODD, LP1, CN, CP, L33, O16, EVEN, L32, M8, E8, D6, L16, EB = range(14)
-    ts(T.ip[:, 1:2], T.ip[:, 0:1], 15, A.bitwise_and, ["ip"], "ip1")
-    ts(T.ip[:, 2:3], T.ip[:, 0:1], 4, A.logical_shift_right, ["ip"], "ip2", 1, A.bitwise_and)
-    cp(cc(LANE), T.ip[:, 1:2], ["ip1"], "lane")
-    cp(cc(ODD), T.ip[:, 2:3], ["ip2"], "odd")
+    LANE, ODD, LP1, CN, CP, L33, O16, EVEN, L32, M8, E8, D6, L16, LQ, LR, L4 = range(16)
     fill(T.br[:, 146:147], 2.0 ** -70, "br2")
     fill(T.br[:, 0:1], -2.0 ** 75, "br")
-    ts(cc(CN), cc(LANE), 0.0625, A.mult, ["lane"], "cn", -1.9375, A.add)
-    ts(cc(CP), cc(LANE), -0.0625, A.mult, ["lane"], "cp", -1.0625, A.add)
+    small = [
+        lambda: ts(T.ip[:, 1:2], T.ip[:, 0:1], 15, A.bitwise_and, ["ip"], "ip1"),
+        lambda: ts(T.ip[:, 2:3], T.ip[:, 0:1], 4, A.logical_shift_right, ["ip"], "ip2", 1, A.bitwise_and),
+        lambda: cp(cc(LANE), T.ip[:, 1:2], ["ip1"], "lane"),
+        lambda: cp(cc(ODD), T.ip[:, 2:3], ["ip2"], "odd"),
+        lambda: ts(T.otb[:, 0:4], T.itb[:, :], cc(LANE), A.add, ["itb", "lane"], "otba"),
+        lambda: ts(T.otb[:, 4:5], cc(LANE), 216.0, A.add, ["lane"], "otbb"),
+        lambda: ts(T.otb[:, 5:6], cc(LANE), 216.0, A.add, ["lane"], "otbc"),
+        lambda: ts(T.otb[:, 6:7], cc(LANE), 17.0, A.mult, ["lane"], "otbd", 17.0, A.add),
+        lambda: ts(T.otb[:, 7:8], cc(LANE), 17.0, A.mult, ["lane"], "otbe", 17.0, A.add),
+        lambda: ts(cc(CN), cc(LANE), 0.0625, A.mult, ["lane"], "cn", -1.9375, A.add),
+        lambda: ts(cc(CP), cc(LANE), -0.0625, A.mult, ["lane"], "cp", -1.0625, A.add),
+        lambda: cp(T.opick[:, :], T.ipick[:, :], ["ipick"], "opick"),
+        lambda: ts(T.off[:, 1:2], cc(LANE), 0.0, A.is_equal, ["lane"], "off1", 8.0, A.mult),
+        lambda: ts(cc(LP1), cc(LANE), 1.0, A.add, ["lane"], "lp1")]
     k = 1
     while k < 146:
         s = min(k, 64)
@@ -154,45 +164,39 @@ def rank_program(g, core, T, topo):
         ts(T.br[:, k:k + n1], T.br[:, k - s:k - s + n1], 2.0 ** -s, A.mult, ["br"], "br")
         if n2 > 0:
             act(T.br[:, 146 + k:146 + k + n2], T.br[:, 146 + k - s:146 + k - s + n2], AF.Identity, ["br2"], ["br2"], scale=2.0 ** s)
+        for f in small[:2]:
+            f()
+        small = small[2:]
         k *= 2
     B = ["br", "br2"]
+    cp(T.tbr[:, :], T.br[:, 0:290].indirect(T.otb[:, :]), B + ["otba", "otbb", "otbc", "otbd", "otbe"], "tbr")
+    do("v", V.transpose, T.tbt[:, :], T.tbr[:, :], r=["tbr"], w=["tbt"])
+    ts(T.tb[:, 0:8], T.br[:, 1:121:17], T.tbt[:, 0:1], A.mult, ["br", "tbt"], "tba")
+    ts(T.tb[:, 9:17], T.br[:, 154:274:17], T.tbt[:, 64:65], A.mult, ["br2", "tbt"], "tbb", -1.0, A.mult)
+    ts(T.tb[:, 8:9], T.tbt[:, 32:33], -1.0, A.mult, ["tbt"], "tbc")
+    ts(T.tb[:, 17:18], T.tbt[:, 96:97], -1.0, A.mult, ["tbt"], "tbd")
     act(T.nt1[:, 0:145], T.br[:, 1:146], AF.Identity, ["br", "cn"], ["nta"], scale=cc(CN))
     act(T.nt1[:, 146:289], T.br[:, 146:289], AF.Identity, ["br2", "cp"], ["ntb"], scale=cc(CP))
     act(T.wt[:, 0:145], T.br[:, 1:146], AF.Identity, ["br"], ["wta"], scale=-1.0)
     act(T.wt[:, 146:289], T.br[:, 146:289], AF.Identity, ["br2"], ["wtb"])
-    act(T.iw[:, 4:145], T.br[:, 146:287], AF.Identity, ["br2"], ["iwa"])
-    act(T.iw[:, 146:287], T.br[:, 5:146], AF.Identity, ["br"], ["iwb"], scale=-1.0)
-    NT, WT, IW = ["nta", "ntb", "ntc", "ntd"], ["wta", "wtb", "wtc", "wtd"], ["iwa", "iwb", "iwc", "iwd", "iwe"]
-    for r in range(6):
-        act(cc(40 + r), T.br[:, 146:147], AF.Identity, ["br2"], ["crow%d" % r], scale=[-2.0 ** 66, -2.0 ** 62, -2.0 ** 58, -2.0 ** 54, 2.0 ** 50, 2.0 ** 47][r])
-        act(cc(48 + r), T.br[:, 146:147], AF.Identity, ["br2"], ["drow%d" % r], scale=[-2.0 ** 74, -2.0 ** 78, -2.0 ** 82, -2.0 ** 86, -2.0 ** 90, 2.0 ** 93][r])
+    act(T.iw[:, 0:145], T.br[:, 142:287], AF.Identity, B, ["iwa"])
+    act(T.iw[:, 146:289], T.br[:, 5:148], AF.Identity, B, ["iwb"], scale=-1.0)
+    NT, WT, IW = ["nta", "ntb", "ntc"], ["wta", "wtb", "wtc"], ["iwa", "iwb", "iwc"]
+    act(T.c[:, 40:44], T.br[:, 79:92:4], AF.Identity, ["br"], ["crow0"])
+    act(T.c[:, 44:46], T.br[:, 95:99:3], AF.Identity, ["br"], ["crow1"], scale=-1.0)
+    act(T.c[:, 48:53], T.br[:, 220:237:4], AF.Identity, ["br2"], ["drow0"], scale=-1.0)
+    act(T.c[:, 53:54], T.br[:, 239:240], AF.Identity, ["br2"], ["drow1"])
 
-    def lin(j, w, src, k, add):
-        act(cc(j), cc(src), AF.Identity, ["lane", "odd"], [w], scale=k, bias=add)
-
-    def const(b, c, n, x, w):
-        act(T[b][:, c:c + n], T.br[:, 0:n], AF.Identity, ["br"], [w], scale=0.0, bias=x)
-    lin(56, "cb", LANE, -0.9375, -0.9375)
-    lin(E8, "e8", LANE, 0.125, -3.875)
-    const("iw", 0, 4, 1.0, "iwc")
-    const("iw", 145, 1, 2.0 ** 69, "iwd")
-    const("iw", 287, 9, 1.0, "iwe")
-    const("wt", 145, 1, 2.0 ** -69, "wtc")
-    const("wt", 289, 7, 1.0, "wtd")
-    const("nt1", 289, 7, 1.0, "ntd")
-    act(T.nt1[:, 145:146], cc(LANE), AF.Identity, ["lane"], ["ntc"], scale=-(2.0 ** -73), bias=7 * 2.0 ** -73)
-    lin(L33, "l33", LANE, 33.0, 0.0)
-    lin(O16, "o16", ODD, 16.0, 0.0)
-    lin(L32, "l32", LANE, 32.0, 0.0)
-    ts(T.otb[:, 0:34], T.itb[:, :], cc(LANE), A.add, ["itb", "lane"], "otba")
-    ts(T.otb[:, 34:35], cc(LANE), 17.0, A.mult, ["lane"], "otbb", 17.0, A.add)
-    ts(T.otb[:, 35:36], cc(LANE), 17.0, A.mult, ["lane"], "otbc", 17.0, A.add)
-    cp(T.opick[:, :], T.ipick[:, :], ["ipick"], "opick")
-    ts(T.off[:, 1:2], cc(LANE), 0.0, A.is_equal, ["lane"], "off1", 8.0, A.mult)
-    ts(cc(LP1), cc(LANE), 1.0, A.add, ["lane"], "lp1")
-    cp(T.tbr[:, :], T.br[:, 0:290].indirect(T.otb[:, :]), B + ["otba", "otbb", "otbc"], "tbr")
-    do("v", V.transpose, T.tbt[:, :], T.tbr[:, :], r=["tbr"], w=["tbt"])
-    ts(T.tb[:, 0:18], T.tbt[:, 0:576:32], -1.0, A.mult, ["tbt"], "tb")
+    def lin(out, w, src, k, add):
+        act(out, cc(src), AF.Identity, ["lane", "odd"], [w], scale=k, bias=add)
+    lin(T.iw[:, 145:146], "iwc", LANE, 0.0, 2.0 ** 69)
+    lin(T.wt[:, 145:146], "wtc", LANE, 0.0, 2.0 ** -69)
+    lin(T.nt1[:, 145:146], "ntc", LANE, -(2.0 ** -73), 7 * 2.0 ** -73)
+    lin(cc(56), "cb", LANE, -0.9375, -0.9375)
+    lin(cc(E8), "e8", LANE, 0.125, -3.875)
+    lin(cc(L33), "l33", LANE, 33.0, 0.0)
+    lin(cc(O16), "o16", ODD, 16.0, 0.0)
+    lin(cc(L32), "l32", LANE, 32.0, 0.0)
     quant("u1", 0, 128, T.tu1, ["tu1"], "qu1")
     cp(words(T.qr1[:, :]), words(T.qu1[:, :]).indirect(T.opick[:, :]), ["qu1", "opick"], "qr1")
     act(T.sr1[:, :], T.su1[:, :].indirect(T.opick[:, :]), AF.Copy, ["qu1", "opick"], ["sr1"])
@@ -213,36 +217,57 @@ def rank_program(g, core, T, topo):
     dma("s", codes(T.qW[:, :]), T.wc[:, :], w=["qW"])
     dma("s", T.sW[:, :], T.ws[:, :], w=["sW"])
 
+    def rows(pb, n, ch, a, b):
+        cp(T.srow[:, a:b], T[pb][:, a:b], [pb], "srow%d" % a)
+        if b == n:
+            dma("s", ch[:, :], T.srow[0:128:16, 0:n], r=["srow0", "srow%d" % a], w=["ch"])
+
     def jobs1():
         ts(cc(M8), cc(LANE), 8.0, A.is_lt, ["lane"], "m8")
         ts(cc(D6), cc(E8), cc(M8), A.mult, ["e8", "m8"], "d6", 4.0, A.add)
         ts(cc(60), cc(D6), cc(LP1), A.subtract, ["d6", "lp1"], "cb5")
         ts(cc(61), cc(D6), -8.0, A.mult, ["d6"], "cb6")
-        fill(T.zero[:, :], 0.0, "zero")
-        fill(T.gs[:, 0:1], 0.0, "gs0")
-        fill(T.es[:, 0:1], 0.0, "es0")
-        yield
-        ts(T.pre[:, :], T.jr[:, :], cc(LANE), A.is_lt, ["jr", "lane"], "prea")
-        ts(T.tr1[:, :], T.kr1[:, :], cc(L32), A.add, ["kr1", "l32"], "tr1")
-        yield
-        tt(T.pre[:, 0:264], T.pre[:, 0:264], T.tot[:, 0:264], A.mult, ["prea", "tot"], "preb")
-        yield
-        tt(T.pre[:, 264:528], T.pre[:, 264:528], T.tot[:, 264:528], A.mult, ["prea", "tot"], "prec")
-        yield
-        fill(T.R1[:, 0:512], 0.0, "R1")
-        quant("u2", 0, 128, T.tu2, ["tu2"], "qu2")
-        yield
-
-    def jobs2():
         fill(T.ones[:, :], 1.0, "ones")
         for b in range(4):
             do("g", g.affine_select, T.te[:, 512 * b:512 * b + 512], T.ones[:, :], [[1, 512]], A.is_equal, 0.0, -b, -4, r=["ones"], w=["te%d" % b])
-        ts(cc(L16), cc(LANE), 16.0, A.mult, ["lane"], "l16")
         yield
-        fill(T.R2[:, 0:256], 0.0, "R2")
+        ts(T.pre[:, :], T.jr[:, :], cc(LANE), A.is_lt, ["jr", "lane"], "prea")
+        yield
+        rows("p1", 512, T.ch1, 0, 256)
+        yield
+        rows("p1", 512, T.ch1, 256, 512)
+        yield
+        for j in range(0, 528, 132):
+            tt(T.pre[:, j:j + 132], T.pre[:, j:j + 132], T.tot[:, j:j + 132], A.mult, ["prea", "tot"], "pre%d" % j)
+            if j == 264:
+                fill(T.zero[:, :], 0.0, "zero")
+                fill(T.gs[:, 0:1], 0.0, "gs0")
+                fill(T.es[:, 0:1], 0.0, "es0")
+            yield
+    PRE = ["pre%d" % j for j in range(0, 528, 132)]
+
+    def jobs2():
+        ts(cc(L16), cc(LANE), 16.0, A.mult, ["lane"], "l16")
         ts(T.tr2[:, :], T.kr2[:, :], cc(L16), A.add, ["kr2", "l16"], "tr2")
         ts(cc(EVEN), cc(ODD), -1.0, A.mult, ["odd"], "even", 1.0, A.add)
-        ts(cc(EB), cc(EVEN), -256.0, A.mult, ["even"], "eb")
+        yield
+        fill(T.R2[:, 0:256], 0.0, "R2")
+        ts(T.ip[:, 3:4], T.ip[:, 1:2], 2, A.logical_shift_right, ["ip1"], "ip3")
+        yield
+        rows("p7", 256, T.ch2, 0, 256)
+        yield
+        ts(T.ip[:, 4:5], T.ip[:, 1:2], 3, A.bitwise_and, ["ip1"], "ip4")
+        cp(cc(LQ), T.ip[:, 3:4], ["ip3"], "lq")
+        quant("E", 0, 128, T.te, ["te0"], "qE0", 0)
+        yield
+        cp(cc(LR), T.ip[:, 4:5], ["ip4"], "lr")
+        quant("E", 128, 128, T.te, ["te1"], "qE1", 512)
+        yield
+        ts(cc(L4), cc(LR), 1024.0, A.add, ["lr"], "l4")
+        quant("E", 256, 128, T.te, ["te2"], "qE2", 1024)
+        yield
+        ts(T.orep[:, :], T.irep[:, :], cc(LQ), A.add, ["irep", "lq"], "orep")
+        quant("E", 384, 128, T.te, ["te3"], "qE3", 1536)
         yield
 
     def search(n, pa, pb, first, ch, jobs):
@@ -258,27 +283,27 @@ def rank_program(g, core, T, topo):
         def answer(j):
             ts(T.off[:, 0:1], sm(j), 0.0, A.is_ge, ["sm%d" % j], "off0")
         for j, (p, w) in enumerate(first):
-            count(T.tb[:, 17:18], j, "tb", p, w)
+            count(T.tb[:, 17:18], j, "tbd", p, w)
         job()
         if len(first) == 2:
             ts(sm(1), sm(0), sm(1), A.add, ["sm0", "sm1"], "sm2", 0.0, A.is_ge)
             ts(T.offb[:, 0:1], sm(1), cc(LP1), A.mult, ["sm2", "lp1"], "offb")
         else:
             ts(T.offb[:, 0:1], sm(0), 0.0, A.is_ge, ["sm0", "lp1"], "offb", cc(LP1), A.mult)
-        cp(T.l64[:, 0:16], T.tb[:, 0:17].indirect(T.offb[:, 0:1]), ["offb", "tb"], "b16")
+        cp(T.l64[:, 0:16], T.tb[:, 0:17].indirect(T.offb[:, 0:1]), ["offb", "tba", "tbb", "tbc"], "b16")
         red(sm(3), T.l64[:, 0:16], A.min, ["b16"], "sm3")
         count(sm(3), 4, "sm3")
         cp(T.l64[:, 64:80], T.seq[:, 0:17].indirect(T.offb[:, 0:1]), ["offb", "seq"], "s16")
         red(sm(5), T.l64[:, 64:80], A.max, ["s16"], "sm5")
-        job()
         answer(4)
         act(T.gj[:, 0:16], T.ft[:, 0:8].indirect(T.off[:, 0:1]), AF.Identity, ["off0"] + FT, ["gj", "sm6"], accum_out=sm(6))
+        job()
         ts(T.offn[:, 0:1], sm(6), sm(5), A.add, ["sm6", "sm5"], "offn")
-        act(T.l64[:, 16:32], T.nt1[:, 0:296].indirect(T.offn[:, 0:1]), AF.Identity, ["offn"] + NT, ["n16"])
-        cp(T.l64[:, 32:48], T.iw[:, 0:296].indirect(T.offn[:, 0:1]), ["offn"] + IW, "i16")
-        cp(T.l64[:, 48:64], T.wt[:, 0:296].indirect(T.offn[:, 0:1]), ["offn"] + WT, "w16")
-        ts(T.si8[:, 0:6], T.c[:, 48:54], T.l64[:, 32:33], A.mult, ["i16"] + ["drow%d" % j for j in range(6)], "si8")
-        ts(T.sc8[:, 0:6], T.c[:, 40:46], T.l64[:, 48:49], A.mult, ["w16"] + ["crow%d" % j for j in range(6)], "sc8")
+        act(T.l64[:, 16:32], T.nt1[:, 0:289].indirect(T.offn[:, 0:1]), AF.Identity, ["offn"] + NT, ["n16"])
+        cp(T.l64[:, 32:48], T.iw[:, 0:289].indirect(T.offn[:, 0:1]), ["offn"] + IW, "i16")
+        cp(T.l64[:, 48:64], T.wt[:, 0:289].indirect(T.offn[:, 0:1]), ["offn"] + WT, "w16")
+        ts(T.si8[:, 0:6], T.c[:, 48:54], T.l64[:, 32:33], A.mult, ["i16", "drow0", "drow1"], "si8")
+        ts(T.sc8[:, 0:6], T.c[:, 40:46], T.l64[:, 48:49], A.mult, ["w16", "crow0", "crow1"], "sc8")
         t, tk = T.l64[:, 16:17], "n16"
         for r in range(6):
             nx = "sm%d" % (16 + r)
@@ -287,11 +312,6 @@ def rank_program(g, core, T, topo):
             if r < 5:
                 count(t, 8 + r, tk)
                 ts(T.ft[:, 8:9], t, T.si8[:, r:r + 1], A.mult, cr, "base", cb, A.add)
-                if r == 1:
-                    cp(T.srow[:, 0:n], T[pb][:, 0:n], [pb], "srow")
-                    dma("s", ch[:, :], T.srow[0:128:16, 0:n], r=["srow"], w=["ch"])
-                elif r > 1:
-                    job()
                 answer(8 + r)
             else:
                 m = n // 2
@@ -303,6 +323,7 @@ def rank_program(g, core, T, topo):
                 ts(T.off[:, 0:1], sm(14), sm(13), A.add, ["sm13", "sm14"], "off0", n / 2.0, A.is_ge)
             act(T.gj[:, 0:32], T.ft[:, :].indirect(T.off[:, 0:2]), AF.Identity, ["off0", "off1", "sc8"] + FT, ["gj", nx], scale=T.sc8[:, r:r + 1], accum_out=sm(16 + r))
             t, tk = sm(16 + r), nx
+            job()
         for _ in jobs:
             pass
         ts(T.gt[:, 0:q], ch[:, :], t, A.is_gt, ["ch", tk], "gt")
@@ -311,21 +332,23 @@ def rank_program(g, core, T, topo):
         do("v", V.tensor_tensor_scan, T.es[:, 1:q + 1], T.eq[:, 0:q], T.zero[:, 0:q], 0.0, A.add, A.add, r=["eq", "zero"], w=["es"])
         ts(T.og[:, 0:1], T.gs[:, q:q + 1], cc(L33), A.add, ["gs", "l33"], "og")
         ts(T.oe[:, 0:1], T.es[:, q:q + 1], cc(L33), A.add, ["es", "l33"], "oe")
-        for tab, o, j in (("tot", "og", 31), ("pre", "og", 30), ("pre", "oe", 32)):
-            act(T.gj[:, 0:16], T[tab][:, :].indirect(T[o][:, 0:1]), AF.Identity, [o] + (["preb", "prec"] if tab == "pre" else ["tot"]), ["gj", "sm%d" % j], accum_out=sm(j))
+        act(T.gj[:, 0:16], T.tot[:, :].indirect(T.og[:, 0:1]), AF.Identity, ["og", "tot"], ["gj", "sm31"], scale=-1.0, bias=n / 32.0, accum_out=sm(31))
+        for o, j in (("oe", 32), ("og", 30)):
+            act(T.gj[:, 16:32] if j == 32 else T.gj[:, 0:16], T.pre[:, :].indirect(T[o][:, 0:1]), AF.Identity, [o] + PRE, ["gk" if j == 32 else "gj", "sm%d" % j], accum_out=sm(j))
+        if n == 512:
+            fill(T.R1[:, 0:512], 0.0, "R1")
+            ts(T.tr1[:, :], T.kr1[:, :], cc(L32), A.add, ["kr1", "l32"], "tr1")
         tr, trk = (T.tr1, "tr1") if n == 512 else (T.tr2, "tr2")
-        ts(sm(33), sm(31), -1.0, A.mult, ["sm31"], "sm33", n / 2.0, A.add)
+        ts(T.me[:, 0:q + 1], T.es[:, 0:q + 1], sm(32), A.add, ["es0", "es", "sm32", "sm31"], "me", sm(31), A.min)
         ts(T.gsg[:, 0:q + 1], T.gs[:, 0:q + 1], sm(30), A.add, ["gs0", "gs", "sm30"], "gsg")
-        ts(T.me[:, 0:q + 1], T.es[:, 0:q + 1], sm(32), A.add, ["es0", "es", "sm32", "sm33"], "me", sm(33), A.min)
-        tt(T.pi[:, 0:q + 1], T.gsg[:, 0:q + 1], T.me[:, 0:q + 1], A.add, ["gsg", "me"], "pi")
-        tt(T.kp[:, 0:q], T.pi[:, 1:q + 1], T.pi[:, 0:q], A.subtract, ["pi"], "kp")
-        tt(T.dd[:, 0:q], T.pi[:, 0:q], tr[:, :], A.subtract, ["pi", trk], "dd")
-        tt(T.mm[:, 0:q], T.dd[:, 0:q], T.kp[:, 0:q], A.mult, ["dd", "kp"], "mm")
-        tt(T.vi[:, 0:q], T.mm[:, 0:q], tr[:, :], A.add, ["mm", trk], "vi")
+        tt(T.vi[:, 0:q + 1], T.gsg[:, 0:q + 1], T.me[:, 0:q + 1], A.add, ["gsg", "me"], "vi")
         ts(T.vq[:, 0:q], T.vi[:, 0:q], 1008, A.bitwise_and, ["vi"], "vq")
+        tt(T.kp[:, 0:q], T.vi[:, 0:q], T.vi[:, 1:q + 1], A.is_ge, ["vi"], "kp")
         tt(T.vg[:, 0:q], T.vi[:, 0:q], T.vq[:, 0:q], A.add, ["vi", "vq"], "vg")
+        tt(T.mm[:, 0:q], T.kp[:, 0:q], tr[:, :], A.mult, ["kp", trk], "mm")
+        tt(T.dd[:, 0:q], T.mm[:, 0:q], T.vg[:, 0:q], A.max, ["mm", "vg"], "dd")
         so, R, rk, val, vk, Tr, W = (T.osc1, T.R1, "R1", T.val1, "val1", T.Tr1, T.W1) if n == 512 else (T.osc2, T.R2, "R2", T.val2, "val2", T.Tr2, T.W2)
-        ts(so[:, :], T.vg[:, 0:q], cc(O16), A.add, ["vg", "o16"], "so")
+        ts(so[:, :], T.dd[:, 0:q], cc(O16), A.add, ["dd", "o16"], "so")
         cp(R[:, :].indirect(so[:, :]), val[:, :], ["so", vk], rk)
         do("v", V.transpose, Tr[:, :], R[:, 0:n], r=[rk], w=["Tr"])
         tt(W[:, :], Tr[:, 0:n:32], Tr[:, 16:n:32], A.add, ["Tr"], "W%d" % n)
@@ -362,8 +385,9 @@ def rank_program(g, core, T, topo):
     dma("s", T.xf[:, :], T.x[:, :], w=["xf"])
     offsets("o1", "W512", T.W1, 16, 1024.0)
     gather("tf", 256, T.tx, X, "o1", 16, "avav")
-    act(T.sr2[:, :], T.su2[:, :].indirect(T.opick[:, :]), AF.Copy, ["qu2", "opick"], ["sr2"])
+    quant("u2", 0, 128, T.tu2, ["tu2"], "qu2")
     quant("F", 0, 256, T.tf, four("tf"), "qF")
+    act(T.sr2[:, :], T.su2[:, :].indirect(T.opick[:, :]), AF.Copy, ["qu2", "opick"], ["sr2"])
     cp(words(T.qr2[:, :]), words(T.qu2[:, :]).indirect(T.opick[:, :]), ["qu2", "opick"], "qr2")
     layer("th", "W", "F", 256, ["qW", "sW", "qF"])
     dma("s", T.txh[:, :], T.tf[:, :], r=four("tf"), w=["txh"])
@@ -409,35 +433,30 @@ def rank_program(g, core, T, topo):
     act(T.L1r[:, :], T.ir[:, :].indirect(T.o1[:, 64:80]), AF.Identity, ["ir", "o1c"], ["L1r"])
     act(T.olr[:, :], T.L1r[:, :].indirect(T.o2[:, 32:40]), AF.Identity, ["L1r", "o2c"], ["olr"])
     dma("s", T.ol[:, :], T.olr[0:128:16, :], r=["olr"], w=["ol"])
+    act(T.gap3[:, :], T.olr[:, :].indirect(T.orep[:, :]), AF.Identity, ["olr", "orep"], ["gap3"], bias=-256.0)
 
     def base(t):
         cp(T.xf[:, :].indirect(T.o1[:, 16 * t:16 * t + 16]), T.txh[:, t:1024:4], ["o1_%d" % t, "txh"], "xf")
     base(0)
-    for b in range(8):
-        i = T.olr[:, 16 * b:16 * b + 16]
-        act(T.gap3[:, 32 * b:32 * b + 16], i, AF.Identity, ["olr", "even", "eb"], ["gap%d" % b], scale=cc(EVEN), bias=cc(EB))
-        ts(T.gap3[:, 32 * b + 16:32 * b + 32], i, -256.0, A.add, ["olr", "odd"], "gap%d" % (8 + b), cc(ODD), A.mult)
-    do("v", V.transpose, T.Tr3[:, :], T.gap3[:, :], r=["gap%d" % b for b in range(16)], w=["Tr3"])
-    tt(T.W3[:, :], T.Tr3[:, 0:256:32], T.Tr3[:, 16:256:32], A.add, ["Tr3"], "W3")
-    offsets("o3", "W3", T.W3, 8, 1024.0)
     base(1)
+    do("v", V.transpose, T.Tr3[:, :], T.gap3[:, :], r=["gap3"], w=["Tr3"])
+    ts(T.W3[:, 0:32], T.Tr3[:, 0:1024:32], cc(EVEN), A.mult, ["Tr3", "even"], "w3a")
+    ts(T.W3[:, 32:64], T.Tr3[:, 16:1024:32], cc(ODD), A.mult, ["Tr3", "odd"], "w3b")
+    tt(T.W3[:, 64:96], T.W3[:, 0:32], T.W3[:, 32:64], A.add, ["w3a", "w3b"], "w3c")
+    ts(T.o3[:, :], T.W3[:, 64:96], 4.0, A.mult, ["w3c", "l4"], "o3", cc(L4), A.add)
     layer("tt", "Z", "L", 128, ["qZ", "sZ", "qGo", "qGp", "qGr"])
     quant("T", 0, 128, T.tt, four("tt"), "qT")
     swap("T", "U", "up")
-    for b in range(4):
-        quant("E", 128 * b, 128, T.te, ["te%d" % b], "qE%d" % b, 512 * b)
+    act(T.txg[:, :], T.tx[:, :].indirect(T.o3[:, :]), AF.Copy, X + ["o3"], ["txg"])
     quant("v", 0, 128, T.tv, ["tv"], "qvv")
     base(2)
     base(3)
-    gather("txg", 128, T.tx, X, "o3", 8, "aaaa")
     for b in range(4):
         mm("p%d" % (2 + b), 128, "E", 128 * b, "U", 0, ["qE%d" % b, "qTo", "qTp", "qTr"])
     for b in range(4):
         tt(T.thn[:, b:512:4], T["p%d" % (2 + b)][:, 0:128], T.tg[:, b:512:4], A.add, ["p%d" % (2 + b), "tg%d" % b], "thn%d" % b)
-    for b in range(4):
-        tt(T.txn[:, b:512:4], T.txg[:, b:512:4], T.thn[:, b:512:4], A.add, ["txg%d" % b, "thn%d" % b], "txn%d" % b)
-    for b in range(4):
-        cp(T.xf[:, :].indirect(T.o3[:, 8 * b:8 * b + 8]), T.txn[:, b:512:4], ["o3_%d" % b, "txn%d" % b], "xf")
+    tt(T.txn[:, :], T.txg[:, :], T.thn[:, :], A.add, ["txg"] + four("thn"), "txn")
+    cp(T.xf[:, :].indirect(T.o3[:, :]), T.txn[:, :], ["o3", "txn"], "xf")
     for h, (c, n) in enumerate(((0, 256), (256, 128), (384, 128))):
         p = "p%d" % h
         quant("N", c, n, T.xf, ["xf"], "qN%d" % h)

@@ -5,11 +5,12 @@ F8, U8, BF, F32, I32, U16 = "float8_e4m3fn_x4", "uint8", "bfloat16", "float32", 
 SCRATCH = {}
 for _d, _l in (
     (BF, "tu1 512 tu2 512 tv 512 tx 2048 xf 2048 tf 1024 th 1024 txh 1024 tg 512 tt 512 thn 512 txg 512 txn 512 ones 512 te 2048 "
-         "tot 528 jr 528 pre 528 val1 512 val2 256 sj 512 sjv 512 R1 1056 R2 544 Tr1 512 Tr2 256 Tr3 1024 gap3 1024 W1 16 W2 8 W3 96"),
-    (F32, "br 296 wt 296 iw 296 nt1 296 tbr 128 tbt 128 tb 24 seq 24 ft 16 ir 512 kr1 32 kr2 16 tr1 32 tr2 16 zero 32 c 64 gj 32 l64 96 "
-          "sc8 8 si8 8 sm 64 srow 512 ch1 32 ch2 16 gt 32 eq 32 gs 36 es 36 gsg 36 me 36 kp 32 dd 32 mm 32 vg 32 L1r 256 olr 128 ysb 512"),
-    (I32, "ip 8 ipick 8 itb 4 irep 64 vi 36 vq 32"),
-    (U16, "opick 8 otb 8 orep 64 off 2 offb 2 offn 2 og 2 oe 2 osc1 32 osc2 16 o1 80 o2 40 o3 32")):
+         "tot 528 ps 1056 val1 512 val2 256 sj 512 sjv 512 R1 1056 R2 544 Tr1 512 Tr2 256 Tr3 1024 gap3 1024 W1 16 W2 8 W3 96"),
+    (F32, "br 296 wt 296 iw 296 nt1 296 tbr 128 tbt 128 tb 24 seq 24 ft 16 ir 512 kr1 32 kr2 16 tr1 32 tr2 16 zero 32 c 64 gj 64 l64 128 "
+          "sc8 8 si8 8 sm 64 srow 512 ch1 32 ch2 16 gt 32 eq 32 lt 32 ges 72 es2 32 ngt 32 trn 32 y1 32 me 32 dd 32 mm 32 vg 32 "
+          "L1r 256 olr 128 ysb 512"),
+    (I32, "ip 8 ipick 8 itb 4 irep 64 vi 32 vq 32"),
+    (U16, "opick 8 otb 8 orep 64 off 2 offb 2 offn 2 offq 2 og 2 osc1 32 osc2 16 o1 80 o2 40 o3 32")):
     _l = _l.split()
     for _i in range(0, len(_l), 2):
         SCRATCH[_l[_i]] = ("sbuf", [128, int(_l[_i + 1])], _d)
@@ -19,7 +20,7 @@ for _n, _w in (("W", 512), ("Z", 512), ("x", 512), ("N", 512), ("E", 512), ("F",
     SCRATCH["s" + _n] = ("sbuf", [128, _w], U8)
 for _i in range(8):
     SCRATCH["p%d" % _i] = ("psum", [128, 512], F32)
-SEMAPHORES = ["qv", "qa", "qt", "qg", "down", "up", "sent"] + ["d%d" % i for i in range(40)]
+SEMAPHORES = ["qv", "qa", "qt", "qg", "down", "up", "sent"] + ["d%d" % i for i in range(44)]
 
 
 def rank_program(g, core, T, topo):
@@ -95,6 +96,9 @@ def rank_program(g, core, T, topo):
     def red(out, in_, op, r, w):
         do("v", V.tensor_reduce, out, in_, AxisListType.X, op, r=r, w=[w])
 
+    def scan(out, a, z, r, w):
+        do("v", V.tensor_tensor_scan, out, a, z, 0.0, A.add, A.add, r=r, w=[w])
+
     def fill(ap, x, w):
         do("v", V.memset, ap, x, w=[w])
 
@@ -127,18 +131,25 @@ def rank_program(g, core, T, topo):
             k *= m
         f = {} if SCRATCH[n][2] == I32 else {"allow_small_or_imprecise_dtypes": True}
         do("g", g.iota, T[n][:, 0:k], pattern, base, cm, w=[n], **f)
+
+    def select(out, src, pattern, op, base, cm, r, w):
+        do("g", g.affine_select, out, src, pattern, op, 0.0, base, cm, r=r, w=[w])
     iota("ip", [[1, 1]], 0, 1)
     iota("itb", [[62, 2], [0, 2]], 75)
     iota("ipick", [[16, 8]], 0)
     iota("seq", [[17, 17]], 0)
-    iota("tot", [[0, 16], [1, 33]], 0)
-    iota("jr", [[1, 16], [0, 33]], 0)
     iota("kr1", [[1, 32]], 512)
-    iota("kr2", [[1, 16]], 256)
+    iota("tot", [[0, 16], [1, 33]], 0)
+    select(T.ps[0:16, 0:528], T.tot[0:16, :], [[-1, 16], [0, 33]], A.is_gt, 0, 1, ["tot"], "psa")
+    select(T.ps[0:16, 528:1056], T.tot[0:16, :], [[1, 16], [0, 33]], A.is_ge, 0, -1, ["tot"], "psb")
     iota("val1", [[1, 32], [32, 16]], -256)
-    iota("irep", [[4, 32], [0, 2]], 0)
+    iota("kr2", [[1, 16]], 256)
     iota("val2", [[1, 16], [16, 16]], 0)
+    iota("irep", [[4, 32], [0, 2]], 0)
     iota("ir", [[1, 512]], 0)
+    iota("ones", [[0, 512]], 1)
+    for b in range(4):
+        select(T.te[:, 512 * b:512 * b + 512], T.ones[:, :], [[1, 512]], A.is_equal, -b, -4, ["ones"], "te%d" % b)
     LANE, ODD, LP1, CN, CP, L33, O16, EVEN, L32, M8, E8, D6, L16, LQ, LR, L4 = range(16)
     fill(T.br[:, 146:147], 2.0 ** -70, "br2")
     fill(T.br[:, 0:1], -2.0 ** 75, "br")
@@ -152,8 +163,8 @@ def rank_program(g, core, T, topo):
         lambda: ts(T.otb[:, 5:6], cc(LANE), 216.0, A.add, ["lane"], "otbc"),
         lambda: ts(T.otb[:, 6:7], cc(LANE), 17.0, A.mult, ["lane"], "otbd", 17.0, A.add),
         lambda: ts(T.otb[:, 7:8], cc(LANE), 17.0, A.mult, ["lane"], "otbe", 17.0, A.add),
-        lambda: ts(cc(CN), cc(LANE), 0.0625, A.mult, ["lane"], "cn", -1.9375, A.add),
-        lambda: ts(cc(CP), cc(LANE), -0.0625, A.mult, ["lane"], "cp", -1.0625, A.add),
+        lambda: ts(cc(CN), cc(LANE), -0.0625, A.mult, ["lane"], "cn", 1.9375, A.add),
+        lambda: ts(cc(CP), cc(LANE), 0.0625, A.mult, ["lane"], "cp", 1.0625, A.add),
         lambda: cp(T.opick[:, :], T.ipick[:, :], ["ipick"], "opick"),
         lambda: ts(T.off[:, 1:2], cc(LANE), 0.0, A.is_equal, ["lane"], "off1", 8.0, A.mult),
         lambda: ts(cc(LP1), cc(LANE), 1.0, A.add, ["lane"], "lp1")]
@@ -163,46 +174,47 @@ def rank_program(g, core, T, topo):
         n1, n2 = min(2 * k, 146) - k, min(2 * k, 144) - k
         ts(T.br[:, k:k + n1], T.br[:, k - s:k - s + n1], 2.0 ** -s, A.mult, ["br"], "br")
         if n2 > 0:
-            act(T.br[:, 146 + k:146 + k + n2], T.br[:, 146 + k - s:146 + k - s + n2], AF.Identity, ["br2"], ["br2"], scale=2.0 ** s)
+            ts(T.br[:, 146 + k:146 + k + n2], T.br[:, 146 + k - s:146 + k - s + n2], 2.0 ** s, A.mult, ["br2"], "br2")
         for f in small[:2]:
             f()
         small = small[2:]
         k *= 2
     B = ["br", "br2"]
+    quant("u1", 0, 128, T.tu1, ["tu1"], "qu1")
     cp(T.tbr[:, :], T.br[:, 0:290].indirect(T.otb[:, :]), B + ["otba", "otbb", "otbc", "otbd", "otbe"], "tbr")
+    cp(words(T.qr1[:, :]), words(T.qu1[:, :]).indirect(T.opick[:, :]), ["qu1", "opick"], "qr1")
     do("v", V.transpose, T.tbt[:, :], T.tbr[:, :], r=["tbr"], w=["tbt"])
-    ts(T.tb[:, 0:8], T.br[:, 1:121:17], T.tbt[:, 0:1], A.mult, ["br", "tbt"], "tba")
-    ts(T.tb[:, 9:17], T.br[:, 154:274:17], T.tbt[:, 64:65], A.mult, ["br2", "tbt"], "tbb", -1.0, A.mult)
-    ts(T.tb[:, 8:9], T.tbt[:, 32:33], -1.0, A.mult, ["tbt"], "tbc")
-    ts(T.tb[:, 17:18], T.tbt[:, 96:97], -1.0, A.mult, ["tbt"], "tbd")
-    act(T.nt1[:, 0:145], T.br[:, 1:146], AF.Identity, ["br", "cn"], ["nta"], scale=cc(CN))
-    act(T.nt1[:, 146:289], T.br[:, 146:289], AF.Identity, ["br2", "cp"], ["ntb"], scale=cc(CP))
-    act(T.wt[:, 0:145], T.br[:, 1:146], AF.Identity, ["br"], ["wta"], scale=-1.0)
-    act(T.wt[:, 146:289], T.br[:, 146:289], AF.Identity, ["br2"], ["wtb"])
-    act(T.iw[:, 0:145], T.br[:, 142:287], AF.Identity, B, ["iwa"])
-    act(T.iw[:, 146:289], T.br[:, 5:148], AF.Identity, B, ["iwb"], scale=-1.0)
+    fill(T.ft[:, 0:16], 0.0, "base")
+    fill(T.ges[:, :], 0.0, "ges0")
+    fill(T.zero[:, :], 0.0, "zero")
+    ts(T.tb[:, 17:18], T.tbt[:, 96:97], 1.0, A.mult, ["tbt"], "tbd")
+    ts(T.tb[:, 18:19], T.tbt[:, 96:97], -1.0, A.mult, ["tbt"], "tbe")
+    ts(T.tb[:, 0:8], T.br[:, 1:121:17], T.tbt[:, 0:1], A.mult, ["br", "tbt"], "tba", -1.0, A.mult)
+    ts(T.tb[:, 9:17], T.br[:, 154:274:17], T.tbt[:, 64:65], A.mult, ["br2", "tbt"], "tbb")
+    ts(T.tb[:, 8:9], T.tbt[:, 32:33], 1.0, A.mult, ["tbt"], "tbc")
+    do("v", V.memset, T.ft[:, 1:2], 1.0, r=["base"], w=["fta"])
+    FT = ["fta", "base"]
     NT, WT, IW = ["nta", "ntb", "ntc"], ["wta", "wtb", "wtc"], ["iwa", "iwb", "iwc"]
-    act(T.c[:, 40:44], T.br[:, 79:92:4], AF.Identity, ["br"], ["crow0"])
-    act(T.c[:, 44:46], T.br[:, 95:99:3], AF.Identity, ["br"], ["crow1"], scale=-1.0)
-    act(T.c[:, 48:53], T.br[:, 220:237:4], AF.Identity, ["br2"], ["drow0"], scale=-1.0)
-    act(T.c[:, 53:54], T.br[:, 239:240], AF.Identity, ["br2"], ["drow1"])
 
     def lin(out, w, src, k, add):
         act(out, cc(src), AF.Identity, ["lane", "odd"], [w], scale=k, bias=add)
     lin(T.iw[:, 145:146], "iwc", LANE, 0.0, 2.0 ** 69)
     lin(T.wt[:, 145:146], "wtc", LANE, 0.0, 2.0 ** -69)
-    lin(T.nt1[:, 145:146], "ntc", LANE, -(2.0 ** -73), 7 * 2.0 ** -73)
+    lin(T.nt1[:, 145:146], "ntc", LANE, 2.0 ** -73, -7 * 2.0 ** -73)
     lin(cc(56), "cb", LANE, -0.9375, -0.9375)
     lin(cc(E8), "e8", LANE, 0.125, -3.875)
     lin(cc(L33), "l33", LANE, 33.0, 0.0)
     lin(cc(O16), "o16", ODD, 16.0, 0.0)
     lin(cc(L32), "l32", LANE, 32.0, 0.0)
-    quant("u1", 0, 128, T.tu1, ["tu1"], "qu1")
-    cp(words(T.qr1[:, :]), words(T.qu1[:, :]).indirect(T.opick[:, :]), ["qu1", "opick"], "qr1")
+    act(T.nt1[:, 0:145], T.br[:, 1:146], AF.Identity, ["br", "cn"], ["nta"], scale=cc(CN))
+    act(T.nt1[:, 146:289], T.br[:, 146:289], AF.Identity, ["br2", "cp"], ["ntb"], scale=cc(CP))
     act(T.sr1[:, :], T.su1[:, :].indirect(T.opick[:, :]), AF.Copy, ["qu1", "opick"], ["sr1"])
-    fill(T.ft[:, 0:16], 0.0, "base")
-    do("v", V.memset, T.ft[:, 1:2], 1.0, r=["base"], w=["fta"])
-    FT = ["fta", "base"]
+    act(T.wt[:, 0:145], T.br[:, 1:146], AF.Identity, ["br"], ["wta"], scale=-1.0)
+    act(T.wt[:, 146:289], T.br[:, 146:289], AF.Identity, ["br2"], ["wtb"])
+    act(T.c[:, 40:44], T.br[:, 79:92:4], AF.Identity, ["br"], ["crow0"], scale=-1.0)
+    act(T.c[:, 44:46], T.br[:, 95:99:3], AF.Identity, ["br"], ["crow1"], scale=-1.0)
+    act(T.c[:, 48:53], T.br[:, 220:237:4], AF.Identity, ["br2"], ["drow0"])
+    act(T.c[:, 53:54], T.br[:, 239:240], AF.Identity, ["br2"], ["drow1"])
 
     for j in range(4):
         quant("x", 128 * j, 128, T.tx, ["tx%d" % j], "qx%d" % j)
@@ -216,6 +228,9 @@ def rank_program(g, core, T, topo):
     dma("s", T.tu2[:, :], T.u2[:, :], w=["tu2"])
     dma("s", codes(T.qW[:, :]), T.wc[:, :], w=["qW"])
     dma("s", T.sW[:, :], T.ws[:, :], w=["sW"])
+    for j in range(1, 8):
+        dma("s", T.ps[16 * j:16 * j + 16, :], T.ps[0:16, :], r=["psa", "psb"], w=["ps%d" % j])
+    PS = ["psa", "psb"] + ["ps%d" % j for j in range(1, 8)]
 
     def rows(pb, n, ch, a, b):
         cp(T.srow[:, a:b], T[pb][:, a:b], [pb], "srow%d" % a)
@@ -224,128 +239,144 @@ def rank_program(g, core, T, topo):
 
     def jobs1():
         ts(cc(M8), cc(LANE), 8.0, A.is_lt, ["lane"], "m8")
+        ts(T.tr1[:, :], T.kr1[:, :], cc(L32), A.add, ["kr1", "l32"], "tr1")
         ts(cc(D6), cc(E8), cc(M8), A.mult, ["e8", "m8"], "d6", 4.0, A.add)
-        ts(cc(60), cc(D6), cc(LP1), A.subtract, ["d6", "lp1"], "cb5")
-        ts(cc(61), cc(D6), -8.0, A.mult, ["d6"], "cb6")
-        fill(T.ones[:, :], 1.0, "ones")
-        for b in range(4):
-            do("g", g.affine_select, T.te[:, 512 * b:512 * b + 512], T.ones[:, :], [[1, 512]], A.is_equal, 0.0, -b, -4, r=["ones"], w=["te%d" % b])
-        yield
-        ts(T.pre[:, :], T.jr[:, :], cc(LANE), A.is_lt, ["jr", "lane"], "prea")
         yield
         rows("p1", 512, T.ch1, 0, 256)
         yield
         rows("p1", 512, T.ch1, 256, 512)
         yield
-        for j in range(0, 528, 132):
-            tt(T.pre[:, j:j + 132], T.pre[:, j:j + 132], T.tot[:, j:j + 132], A.mult, ["prea", "tot"], "pre%d" % j)
-            if j == 264:
-                fill(T.zero[:, :], 0.0, "zero")
-                fill(T.gs[:, 0:1], 0.0, "gs0")
-                fill(T.es[:, 0:1], 0.0, "es0")
-            yield
-    PRE = ["pre%d" % j for j in range(0, 528, 132)]
+        ts(cc(60), cc(D6), cc(LP1), A.subtract, ["d6", "lp1"], "cb5")
+        ts(cc(61), cc(D6), -8.0, A.mult, ["d6"], "cb6")
+        quant("u2", 0, 128, T.tu2, ["tu2"], "qu2")
+        yield
+        cp(words(T.qr2[:, :]), words(T.qu2[:, :]).indirect(T.opick[:, :]), ["qu2", "opick"], "qr2")
+        yield
+        cp(T.sr2[:, :], T.su2[:, :].indirect(T.opick[:, :]), ["qu2", "opick"], "sr2")
+        yield
+        fill(T.R1[:, 0:512], 0.0, "R1")
+        yield
 
     def jobs2():
         ts(cc(L16), cc(LANE), 16.0, A.mult, ["lane"], "l16")
-        ts(T.tr2[:, :], T.kr2[:, :], cc(L16), A.add, ["kr2", "l16"], "tr2")
-        ts(cc(EVEN), cc(ODD), -1.0, A.mult, ["odd"], "even", 1.0, A.add)
-        yield
-        fill(T.R2[:, 0:256], 0.0, "R2")
         ts(T.ip[:, 3:4], T.ip[:, 1:2], 2, A.logical_shift_right, ["ip1"], "ip3")
+        ts(T.ip[:, 4:5], T.ip[:, 1:2], 3, A.bitwise_and, ["ip1"], "ip4")
+        quant("E", 0, 128, T.te, ["te0"], "qE0", 0)
+        yield
+        quant("v", 0, 128, T.tv, ["tv"], "qvv")
+        ts(T.tr2[:, :], T.kr2[:, :], cc(L16), A.add, ["kr2", "l16"], "tr2")
+        cp(cc(LQ), T.ip[:, 3:4], ["ip3"], "lq")
+        cp(cc(LR), T.ip[:, 4:5], ["ip4"], "lr")
         yield
         rows("p7", 256, T.ch2, 0, 256)
         yield
-        ts(T.ip[:, 4:5], T.ip[:, 1:2], 3, A.bitwise_and, ["ip1"], "ip4")
-        cp(cc(LQ), T.ip[:, 3:4], ["ip3"], "lq")
-        quant("E", 0, 128, T.te, ["te0"], "qE0", 0)
-        yield
-        cp(cc(LR), T.ip[:, 4:5], ["ip4"], "lr")
         quant("E", 128, 128, T.te, ["te1"], "qE1", 512)
         yield
-        ts(cc(L4), cc(LR), 1024.0, A.add, ["lr"], "l4")
         quant("E", 256, 128, T.te, ["te2"], "qE2", 1024)
         yield
-        ts(T.orep[:, :], T.irep[:, :], cc(LQ), A.add, ["irep", "lq"], "orep")
         quant("E", 384, 128, T.te, ["te3"], "qE3", 1536)
         yield
+        ts(cc(EVEN), cc(ODD), -1.0, A.mult, ["odd"], "even", 1.0, A.add)
+        ts(cc(L4), cc(LR), 1024.0, A.add, ["lr"], "l4")
+        ts(T.orep[:, :], T.irep[:, :], cc(LQ), A.add, ["irep", "lq"], "orep")
+        fill(T.R2[:, 0:256], 0.0, "R2")
+        yield
 
-    def search(n, pa, pb, first, ch, jobs):
+    def search(n, pa, pb, first, b, ch, jobs):
         q = n // 16
 
         def job():
             for _ in jobs:
                 return
 
-        def count(bias, j, r, p=pa, w=n):
-            act(T.sj[:, 0:w], T[p][:, 0:w], AF.Sign, [p, r], ["sj", "sm%d" % j], bias=bias, accum_out=sm(j))
+        def count(t, j, tk, p, w, sign=-1.0):
+            act(T.sj[:, 0:w], T[p][:, 0:w], AF.Sign, [p, tk], ["sj", "sm%d" % j], scale=sign, bias=t, accum_out=sm(j))
 
-        def answer(j):
-            ts(T.off[:, 0:1], sm(j), 0.0, A.is_ge, ["sm%d" % j], "off0")
-        for j, (p, w) in enumerate(first):
-            count(T.tb[:, 17:18], j, "tbd", p, w)
-        job()
-        if len(first) == 2:
-            ts(sm(1), sm(0), sm(1), A.add, ["sm0", "sm1"], "sm2", 0.0, A.is_ge)
-            ts(T.offb[:, 0:1], sm(1), cc(LP1), A.mult, ["sm2", "lp1"], "offb")
+        def answer(j, n2=0):
+            if n2:
+                ts(T.off[:, 0:1], sm(14), sm(j), A.subtract, ["sm14", "sm%d" % j], "off0", float(n2), A.is_ge)
+            else:
+                ts(T.off[:, 0:1], sm(j), 0.0, A.is_le, ["sm%d" % j], "off0")
+        if first:
+            (p0, w0), (p1, w1) = first
+            count(T.tb[:, 18:19], 1, "tbe", p0, w0, 1.0)
+            count(T.tb[:, 17:18], 0, "tbd", p1, w1)
+            cp(T.iw[:, 0:145], T.br[:, 142:287], B, "iwa")
+            ts(T.iw[:, 146:289], T.br[:, 5:148], -1.0, A.mult, B, "iwb")
         else:
-            ts(T.offb[:, 0:1], sm(0), 0.0, A.is_ge, ["sm0", "lp1"], "offb", cc(LP1), A.mult)
-        cp(T.l64[:, 0:16], T.tb[:, 0:17].indirect(T.offb[:, 0:1]), ["offb", "tba", "tbb", "tbc"], "b16")
-        red(sm(3), T.l64[:, 0:16], A.min, ["b16"], "sm3")
-        count(sm(3), 4, "sm3")
-        cp(T.l64[:, 64:80], T.seq[:, 0:17].indirect(T.offb[:, 0:1]), ["offb", "seq"], "s16")
-        red(sm(5), T.l64[:, 64:80], A.max, ["s16"], "sm5")
-        answer(4)
-        act(T.gj[:, 0:16], T.ft[:, 0:8].indirect(T.off[:, 0:1]), AF.Identity, ["off0"] + FT, ["gj", "sm6"], accum_out=sm(6))
+            fill(sm(1), 0.0, "sm1")
+            count(T.tb[:, 17:18], 0, "tbd", pa, n)
         job()
+        ts(T.offb[:, 0:1], sm(0), sm(1), A.is_le, ["sm0", "sm1", "lp1"], "offb", cc(LP1), A.mult)
+        cp(T.l64[:, 0:16], T.tb[:, 0:17].indirect(T.offb[:, 0:1]), ["offb", "tba", "tbb", "tbc"], "b16")
+        cp(T.l64[:, 64:80], T.seq[:, 0:17].indirect(T.offb[:, 0:1]), ["offb", "seq"], "s16")
+        red(sm(3), T.l64[:, 0:16], A.max, ["b16"], "sm3")
+        red(sm(5), T.l64[:, 64:80], A.max, ["s16"], "sm5")
+        count(sm(3), 4, "sm3", pa, n)
+        ts(sm(2), cc(LP1), sm(5), A.add, ["lp1", "sm5"], "sm2")
+        cp(T.offq[:, 1:2], sm(5), ["sm5"], "offq1")
+        ts(T.offq[:, 0:1], sm(4), 0.0, A.is_le, ["sm4", "sm2"], "offq0", sm(2), A.mult)
+        answer(4)
+        cp(T.l64[:, 96:128], T.nt1[:, 0:289].indirect(T.offq[:, 0:2]), ["offq0", "offq1"] + NT, "n32")
+        act(T.gj[:, 0:16], T.ft[:, 0:8].indirect(T.off[:, 0:1]), AF.Identity, ["off0"] + FT, ["gj", "sm6"], accum_out=sm(6))
+        red(sm(7), T.l64[:, 96:128], A.max, ["n32"], "sm7")
         ts(T.offn[:, 0:1], sm(6), sm(5), A.add, ["sm6", "sm5"], "offn")
-        act(T.l64[:, 16:32], T.nt1[:, 0:289].indirect(T.offn[:, 0:1]), AF.Identity, ["offn"] + NT, ["n16"])
         cp(T.l64[:, 32:48], T.iw[:, 0:289].indirect(T.offn[:, 0:1]), ["offn"] + IW, "i16")
         cp(T.l64[:, 48:64], T.wt[:, 0:289].indirect(T.offn[:, 0:1]), ["offn"] + WT, "w16")
-        ts(T.si8[:, 0:6], T.c[:, 48:54], T.l64[:, 32:33], A.mult, ["i16", "drow0", "drow1"], "si8")
-        ts(T.sc8[:, 0:6], T.c[:, 40:46], T.l64[:, 48:49], A.mult, ["w16", "crow0", "crow1"], "sc8")
-        t, tk = T.l64[:, 16:17], "n16"
+        t, tk = sm(7), "sm7"
         for r in range(6):
             nx = "sm%d" % (16 + r)
-            cb = cc(56 if r < 4 else 56 + r)
-            cr = [tk, "si8", ["cb", "cb5", "cb6"][max(r - 3, 0)]]
-            if r < 5:
-                count(t, 8 + r, tk)
-                ts(T.ft[:, 8:9], t, T.si8[:, r:r + 1], A.mult, cr, "base", cb, A.add)
-                answer(8 + r)
+
+            def base():
+                ts(T.ft[:, 8:9], t, T.si8[:, r:r + 1], A.mult, [tk, "si8", ["cb", "cb5", "cb6"][max(r - 3, 0)]], "base", cc(56 if r < 4 else 56 + r), A.add)
+            if r == 0:
+                count(t, 8, tk, pa, n)
+                ts(T.si8[:, 0:6], T.c[:, 48:54], T.l64[:, 32:33], A.mult, ["i16", "drow0", "drow1"], "si8")
+                if n < 512:
+                    answer(8)
+                ts(T.sc8[:, 0:6], T.c[:, 40:46], T.l64[:, 48:49], A.mult, ["w16", "crow0", "crow1"], "sc8")
+                base()
+                if n == 512:
+                    answer(8)
+            elif r < 5:
+                count(t, 8 + r, tk, pa, n - b)
+                if b:
+                    ts(T.sjv[:, 0:b], T[pb][:, n - b:n], t, A.is_ge, [pb, tk], "sjv0", 2.0, A.mult)
+                base()
+                if b:
+                    red(sm(14), T.sjv[:, 0:b], A.add, ["sjv0"], "sm14")
+                answer(8 + r, b)
             else:
                 m = n // 2
                 ts(T.sjv[:, 0:m], T[pb][:, 0:m], t, A.is_ge, [pb, tk], "sjv0")
                 ts(T.sjv[:, m:n], T[pb][:, m:n], t, A.is_ge, [pb, tk], "sjv1")
                 act(T.sj[:, 0:m], T.sjv[:, 0:m], AF.Copy, ["sjv0"], ["sj", "sm13"], accum_out=sm(13))
+                base()
                 red(sm(14), T.sjv[:, m:n], A.add, ["sjv1"], "sm14")
-                ts(T.ft[:, 8:9], t, T.si8[:, r:r + 1], A.mult, cr, "base", cb, A.add)
                 ts(T.off[:, 0:1], sm(14), sm(13), A.add, ["sm13", "sm14"], "off0", n / 2.0, A.is_ge)
             act(T.gj[:, 0:32], T.ft[:, :].indirect(T.off[:, 0:2]), AF.Identity, ["off0", "off1", "sc8"] + FT, ["gj", nx], scale=T.sc8[:, r:r + 1], accum_out=sm(16 + r))
             t, tk = sm(16 + r), nx
             job()
         for _ in jobs:
             pass
+        tr, trk = (T.tr1, "tr1") if n == 512 else (T.tr2, "tr2")
         ts(T.gt[:, 0:q], ch[:, :], t, A.is_gt, ["ch", tk], "gt")
         ts(T.eq[:, 0:q], ch[:, :], t, A.is_equal, ["ch", tk], "eq")
-        do("v", V.tensor_tensor_scan, T.gs[:, 1:q + 1], T.gt[:, 0:q], T.zero[:, 0:q], 0.0, A.add, A.add, r=["gt", "zero"], w=["gs"])
-        do("v", V.tensor_tensor_scan, T.es[:, 1:q + 1], T.eq[:, 0:q], T.zero[:, 0:q], 0.0, A.add, A.add, r=["eq", "zero"], w=["es"])
-        ts(T.og[:, 0:1], T.gs[:, q:q + 1], cc(L33), A.add, ["gs", "l33"], "og")
-        ts(T.oe[:, 0:1], T.es[:, q:q + 1], cc(L33), A.add, ["es", "l33"], "oe")
-        act(T.gj[:, 0:16], T.tot[:, :].indirect(T.og[:, 0:1]), AF.Identity, ["og", "tot"], ["gj", "sm31"], scale=-1.0, bias=n / 32.0, accum_out=sm(31))
-        for o, j in (("oe", 32), ("og", 30)):
-            act(T.gj[:, 16:32] if j == 32 else T.gj[:, 0:16], T.pre[:, :].indirect(T[o][:, 0:1]), AF.Identity, [o] + PRE, ["gk" if j == 32 else "gj", "sm%d" % j], accum_out=sm(j))
-        if n == 512:
-            fill(T.R1[:, 0:512], 0.0, "R1")
-            ts(T.tr1[:, :], T.kr1[:, :], cc(L32), A.add, ["kr1", "l32"], "tr1")
-        tr, trk = (T.tr1, "tr1") if n == 512 else (T.tr2, "tr2")
-        ts(T.me[:, 0:q + 1], T.es[:, 0:q + 1], sm(32), A.add, ["es0", "es", "sm32", "sm31"], "me", sm(31), A.min)
-        ts(T.gsg[:, 0:q + 1], T.gs[:, 0:q + 1], sm(30), A.add, ["gs0", "gs", "sm30"], "gsg")
-        tt(T.vi[:, 0:q + 1], T.gsg[:, 0:q + 1], T.me[:, 0:q + 1], A.add, ["gsg", "me"], "vi")
+        scan(T.ges[:, 1:q + 1], T.gt[:, 0:q], T.zero[:, 0:q], ["gt", "zero", "ges0"], "gs")
+        scan(T.ges[:, 37:q + 37], T.eq[:, 0:q], T.zero[:, 0:q], ["eq", "zero", "ges0"], "es")
+        ts(T.lt[:, 0:q], ch[:, :], t, A.is_lt, ["ch", tk], "lt", 1024.0, A.mult)
+        ts(T.og[:, 0:2], T.ges[:, q:q + 37:36], cc(L33), A.add, ["gs", "es", "l33"], "og")
+        act(T.gj[:, 0:16], T.ps[:, 528:1056].indirect(T.og[:, 0:1]), AF.Identity, ["og"] + PS, ["gj", "sm31"], scale=-1.0, bias=n / 32.0, accum_out=sm(31))
+        act(T.gj[:, 32:64], T.ps[:, 0:528].indirect(T.og[:, 0:2]), AF.Identity, ["og"] + PS, ["gk", "sm32"], accum_out=sm(32))
+        ts(T.ngt[:, 0:q], ch[:, :], t, A.is_le, ["ch", tk], "ngt")
+        tt(T.es2[:, 0:q], T.ges[:, 36:q + 36], T.lt[:, 0:q], A.add, ["es", "ges0", "lt"], "es2")
+        tt(T.trn[:, 0:q], T.ngt[:, 0:q], tr[:, :], A.mult, ["ngt", trk], "trn")
+        ts(T.me[:, 0:q], T.es2[:, 0:q], sm(32), A.add, ["es2", "sm32", "sm31"], "me", sm(31), A.min)
+        ts(T.y1[:, 0:q], T.es2[:, 0:q], sm(32), A.add, ["es2", "sm32", "sm31"], "y1", sm(31), A.is_ge)
+        tt(T.vi[:, 0:q], T.ges[:, 0:q], T.me[:, 0:q], A.add, ["gs", "ges0", "me"], "vi")
+        tt(T.mm[:, 0:q], T.y1[:, 0:q], T.trn[:, 0:q], A.mult, ["y1", "trn"], "mm")
         ts(T.vq[:, 0:q], T.vi[:, 0:q], 1008, A.bitwise_and, ["vi"], "vq")
-        tt(T.kp[:, 0:q], T.vi[:, 0:q], T.vi[:, 1:q + 1], A.is_ge, ["vi"], "kp")
         tt(T.vg[:, 0:q], T.vi[:, 0:q], T.vq[:, 0:q], A.add, ["vi", "vq"], "vg")
-        tt(T.mm[:, 0:q], T.kp[:, 0:q], tr[:, :], A.mult, ["kp", trk], "mm")
         tt(T.dd[:, 0:q], T.mm[:, 0:q], T.vg[:, 0:q], A.max, ["mm", "vg"], "dd")
         so, R, rk, val, vk, Tr, W = (T.osc1, T.R1, "R1", T.val1, "val1", T.Tr1, T.W1) if n == 512 else (T.osc2, T.R2, "R2", T.val2, "val2", T.Tr2, T.W2)
         ts(so[:, :], T.dd[:, 0:q], cc(O16), A.add, ["dd", "o16"], "so")
@@ -378,24 +409,21 @@ def rank_program(g, core, T, topo):
     def four(n):
         return ["%s%d" % (n, t) for t in range(4)]
 
-    search(512, "p0", "p1", [("p2", 384), ("p3", 128)], T.ch1, jobs1())
+    search(512, "p0", "p1", (("p2", 384), ("p3", 128)), 64, T.ch1, jobs1())
+    dma("s", T.tv[:, :], T.v[:, :], w=["tv"])
     dma("s", codes(T.qZ[:, :]), T.zc[:, :], w=["qZ"])
     dma("s", T.sZ[:, :], T.zs[:, :], w=["sZ"])
-    dma("s", T.tv[:, :], T.v[:, :], w=["tv"])
     dma("s", T.xf[:, :], T.x[:, :], w=["xf"])
     offsets("o1", "W512", T.W1, 16, 1024.0)
     gather("tf", 256, T.tx, X, "o1", 16, "avav")
-    quant("u2", 0, 128, T.tu2, ["tu2"], "qu2")
     quant("F", 0, 256, T.tf, four("tf"), "qF")
-    act(T.sr2[:, :], T.su2[:, :].indirect(T.opick[:, :]), AF.Copy, ["qu2", "opick"], ["sr2"])
-    cp(words(T.qr2[:, :]), words(T.qu2[:, :]).indirect(T.opick[:, :]), ["qu2", "opick"], "qr2")
     layer("th", "W", "F", 256, ["qW", "sW", "qF"])
     dma("s", T.txh[:, :], T.tf[:, :], r=four("tf"), w=["txh"])
     dma("g", T.txh[:, :], T.th[:, :], r=four("th"), w=["txh"], accum_op=A.add)
     quant("H", 0, 256, T.th, four("th"), "qH")
     for p in ("p6", "p7"):
         mm(p, 256, "r2", 0, "H", 0, ["qH", "qr2", "sr2"])
-    search(256, "p6", "p7", [("p6", 256)], T.ch2, jobs2())
+    search(256, "p6", "p7", None, 0, T.ch2, jobs2())
     offsets("o2", "W256", T.W2, 8, 0.0)
     gather("tg", 128, T.th, four("th"), "o2", 8, "avav")
     quant("G", 0, 128, T.tg, four("tg"), "qG")
@@ -439,31 +467,31 @@ def rank_program(g, core, T, topo):
         cp(T.xf[:, :].indirect(T.o1[:, 16 * t:16 * t + 16]), T.txh[:, t:1024:4], ["o1_%d" % t, "txh"], "xf")
     base(0)
     base(1)
+    layer("tt", "Z", "L", 128, ["qZ", "sZ", "qGo", "qGp", "qGr"])
+    quant("T", 0, 128, T.tt, four("tt"), "qT")
+    swap("T", "U", "up")
     do("v", V.transpose, T.Tr3[:, :], T.gap3[:, :], r=["gap3"], w=["Tr3"])
     ts(T.W3[:, 0:32], T.Tr3[:, 0:1024:32], cc(EVEN), A.mult, ["Tr3", "even"], "w3a")
     ts(T.W3[:, 32:64], T.Tr3[:, 16:1024:32], cc(ODD), A.mult, ["Tr3", "odd"], "w3b")
     tt(T.W3[:, 64:96], T.W3[:, 0:32], T.W3[:, 32:64], A.add, ["w3a", "w3b"], "w3c")
     ts(T.o3[:, :], T.W3[:, 64:96], 4.0, A.mult, ["w3c", "l4"], "o3", cc(L4), A.add)
-    layer("tt", "Z", "L", 128, ["qZ", "sZ", "qGo", "qGp", "qGr"])
-    quant("T", 0, 128, T.tt, four("tt"), "qT")
-    swap("T", "U", "up")
     act(T.txg[:, :], T.tx[:, :].indirect(T.o3[:, :]), AF.Copy, X + ["o3"], ["txg"])
-    quant("v", 0, 128, T.tv, ["tv"], "qvv")
     base(2)
     base(3)
     for b in range(4):
         mm("p%d" % (2 + b), 128, "E", 128 * b, "U", 0, ["qE%d" % b, "qTo", "qTp", "qTr"])
     for b in range(4):
         tt(T.thn[:, b:512:4], T["p%d" % (2 + b)][:, 0:128], T.tg[:, b:512:4], A.add, ["p%d" % (2 + b), "tg%d" % b], "thn%d" % b)
-    tt(T.txn[:, :], T.txg[:, :], T.thn[:, :], A.add, ["txg"] + four("thn"), "txn")
-    cp(T.xf[:, :].indirect(T.o3[:, :]), T.txn[:, :], ["o3", "txn"], "xf")
+    for b in range(4):
+        tt(T.txn[:, b:512:4], T.txg[:, b:512:4], T.thn[:, b:512:4], A.add, ["txg", "thn%d" % b], "txn%d" % b)
+    cp(T.xf[:, :].indirect(T.o3[:, :]), T.txn[:, :], ["o3"] + four("txn"), "xf")
     for h, (c, n) in enumerate(((0, 256), (256, 128), (384, 128))):
         p = "p%d" % h
         quant("N", c, n, T.xf, ["xf"], "qN%d" % h)
         mm(p, n, "v", 0, "N", c, ["qvv", "qN%d" % h])
     for h, (c, n) in enumerate(((0, 256), (256, 128), (384, 128))):
         o, i = T.ysb[:, c:c + n], T["p%d" % h][:, 0:n]
-        if h < 2:
+        if h < 1:
             act(o, i, AF.Copy, ["p%d" % h], ["y%d" % h])
         else:
             cp(o, i, ["p%d" % h], "y%d" % h)

@@ -5,12 +5,12 @@ F8, U8, BF, F32, I32, U16 = "float8_e4m3fn_x4", "uint8", "bfloat16", "float32", 
 SCRATCH = {}
 for _d, _l in (
     (BF, "tu1 512 tu2 512 tv 512 tx 2048 xf 2048 tf 1024 th 1024 txh 1024 tg 512 tt 512 thn 512 txg 512 txn 512 ones 512 te 2048 "
-         "tot 528 ps 1056 val1 512 val2 256 sj 512 sjv 512 R1 1056 R2 544 Tr1 512 Tr2 256 Tr3 1024 gap3 1024 W1 16 W2 8 W3 96"),
+         "tot 528 ps 1056 val1 512 val2 256 sj 512 sk 512 sjv 512 R1 1056 R2 544 Tr1 512 Tr2 256 Tr3 1024 gap3 528"),
     (F32, "br 296 wt 296 iw 296 nt1 296 tbr 128 tbt 128 tb 24 seq 24 ft 16 ir 512 kr1 32 kr2 16 tr1 32 tr2 16 zero 32 c 64 gj 64 l64 128 "
-          "sc8 8 si8 8 sm 64 srow 512 ch1 32 ch2 16 gt 32 eq 32 lt 32 ges 72 es2 32 ngt 32 trn 32 y1 32 me 32 dd 32 mm 32 vg 32 "
+          "sc8 8 si8 8 sm 64 srow 512 ch1 32 ch2 16 gt 32 eq 32 lt 32 ges 72 es2 32 ngt 32 trn 32 y1 32 me 32 dd 32 mm 32 vi 32 "
           "L1r 256 olr 128 ysb 512"),
-    (I32, "ip 8 ipick 8 itb 4 irep 64 vi 32 vq 32"),
-    (U16, "opick 8 otb 8 orep 64 off 2 offb 2 offn 2 offq 2 og 2 osc1 32 osc2 16 o1 80 o2 40 o3 32")):
+    (I32, "ip 8 ipick 8 itb 4 irep 33"),
+    (U16, "opick 8 otb 8 orep 34 off 2 offb 2 offn 2 offq 2 og 2 osc1 32 osc2 16 o1 80 o2 80 o3 32 sel1 2 sel2 2 sel3 2")):
     _l = _l.split()
     for _i in range(0, len(_l), 2):
         SCRATCH[_l[_i]] = ("sbuf", [128, int(_l[_i + 1])], _d)
@@ -99,6 +99,9 @@ def rank_program(g, core, T, topo):
     def scan(out, a, z, r, w):
         do("v", V.tensor_tensor_scan, out, a, z, 0.0, A.add, A.add, r=r, w=[w])
 
+    def turn(out, in_, r, w):
+        do("v", V.transpose, out, in_, r=r, w=[w])
+
     def fill(ap, x, w):
         do("v", V.memset, ap, x, w=[w])
 
@@ -145,82 +148,103 @@ def rank_program(g, core, T, topo):
     iota("val1", [[1, 32], [32, 16]], -256)
     iota("kr2", [[1, 16]], 256)
     iota("val2", [[1, 16], [16, 16]], 0)
-    iota("irep", [[4, 32], [0, 2]], 0)
+    iota("irep", [[4, 33]], 0)
     iota("ir", [[1, 512]], 0)
     iota("ones", [[0, 512]], 1)
     for b in range(4):
         select(T.te[:, 512 * b:512 * b + 512], T.ones[:, :], [[1, 512]], A.is_equal, -b, -4, ["ones"], "te%d" % b)
-    LANE, ODD, LP1, CN, CP, L33, O16, EVEN, L32, M8, E8, D6, L16, LQ, LR, L4 = range(16)
-    fill(T.br[:, 146:147], 2.0 ** -70, "br2")
-    fill(T.br[:, 0:1], -2.0 ** 75, "br")
-    small = [
-        lambda: ts(T.ip[:, 1:2], T.ip[:, 0:1], 15, A.bitwise_and, ["ip"], "ip1"),
-        lambda: ts(T.ip[:, 2:3], T.ip[:, 0:1], 4, A.logical_shift_right, ["ip"], "ip2", 1, A.bitwise_and),
-        lambda: cp(cc(LANE), T.ip[:, 1:2], ["ip1"], "lane"),
-        lambda: cp(cc(ODD), T.ip[:, 2:3], ["ip2"], "odd"),
-        lambda: ts(T.otb[:, 0:4], T.itb[:, :], cc(LANE), A.add, ["itb", "lane"], "otba"),
-        lambda: ts(T.otb[:, 4:5], cc(LANE), 216.0, A.add, ["lane"], "otbb"),
-        lambda: ts(T.otb[:, 5:6], cc(LANE), 216.0, A.add, ["lane"], "otbc"),
-        lambda: ts(T.otb[:, 6:7], cc(LANE), 17.0, A.mult, ["lane"], "otbd", 17.0, A.add),
-        lambda: ts(T.otb[:, 7:8], cc(LANE), 17.0, A.mult, ["lane"], "otbe", 17.0, A.add),
-        lambda: ts(cc(CN), cc(LANE), -0.0625, A.mult, ["lane"], "cn", 1.9375, A.add),
-        lambda: ts(cc(CP), cc(LANE), 0.0625, A.mult, ["lane"], "cp", 1.0625, A.add),
-        lambda: cp(T.opick[:, :], T.ipick[:, :], ["ipick"], "opick"),
-        lambda: ts(T.off[:, 1:2], cc(LANE), 0.0, A.is_equal, ["lane"], "off1", 8.0, A.mult),
-        lambda: ts(cc(LP1), cc(LANE), 1.0, A.add, ["lane"], "lp1")]
-    k = 1
-    while k < 146:
-        s = min(k, 64)
-        n1, n2 = min(2 * k, 146) - k, min(2 * k, 144) - k
-        ts(T.br[:, k:k + n1], T.br[:, k - s:k - s + n1], 2.0 ** -s, A.mult, ["br"], "br")
-        if n2 > 0:
-            ts(T.br[:, 146 + k:146 + k + n2], T.br[:, 146 + k - s:146 + k - s + n2], 2.0 ** s, A.mult, ["br2"], "br2")
-        for f in small[:2]:
-            f()
-        small = small[2:]
-        k *= 2
-    B = ["br", "br2"]
-    quant("u1", 0, 128, T.tu1, ["tu1"], "qu1")
-    cp(T.tbr[:, :], T.br[:, 0:290].indirect(T.otb[:, :]), B + ["otba", "otbb", "otbc", "otbd", "otbe"], "tbr")
-    cp(words(T.qr1[:, :]), words(T.qu1[:, :]).indirect(T.opick[:, :]), ["qu1", "opick"], "qr1")
-    do("v", V.transpose, T.tbt[:, :], T.tbr[:, :], r=["tbr"], w=["tbt"])
-    fill(T.ft[:, 0:16], 0.0, "base")
-    fill(T.ges[:, :], 0.0, "ges0")
-    fill(T.zero[:, :], 0.0, "zero")
-    ts(T.tb[:, 17:18], T.tbt[:, 96:97], 1.0, A.mult, ["tbt"], "tbd")
-    ts(T.tb[:, 18:19], T.tbt[:, 96:97], -1.0, A.mult, ["tbt"], "tbe")
-    ts(T.tb[:, 0:8], T.br[:, 1:121:17], T.tbt[:, 0:1], A.mult, ["br", "tbt"], "tba", -1.0, A.mult)
-    ts(T.tb[:, 9:17], T.br[:, 154:274:17], T.tbt[:, 64:65], A.mult, ["br2", "tbt"], "tbb")
-    ts(T.tb[:, 8:9], T.tbt[:, 32:33], 1.0, A.mult, ["tbt"], "tbc")
-    do("v", V.memset, T.ft[:, 1:2], 1.0, r=["base"], w=["fta"])
-    FT = ["fta", "base"]
-    NT, WT, IW = ["nta", "ntb", "ntc"], ["wta", "wtb", "wtc"], ["iwa", "iwb", "iwc"]
+    LANE, ODD, LP1, CN, CP, L33, O16, EVEN, L32, M8, E8, D6, L16, LQ, LR, L4, LB, SO, SO7, L7, LQ4 = range(21)
+    B1, B2 = [], []
 
     def lin(out, w, src, k, add):
         act(out, cc(src), AF.Identity, ["lane", "odd"], [w], scale=k, bias=add)
+
+    def neg(k, n, s):
+        ts(T.br[:, k:k + n], T.br[:, k - s:k - s + n], 2.0 ** -s, A.mult, list(B1), "bn%d" % k)
+
+    def pos(k, n, s):
+        act(T.br[:, 146 + k:146 + k + n], T.br[:, 146 + k - s:146 + k - s + n], AF.Identity, list(B2), ["bp%d" % k], scale=2.0 ** s)
+
+    def grow(f, B, n, parts):
+        for p in parts:
+            f(*p)
+        B += [n + "%d" % p[0] for p in parts]
+    for k in range(4):
+        fill(T.br[:, 146 + k:147 + k], 2.0 ** (k - 70), "bp%d" % k)
+        B2.append("bp%d" % k)
+    for k in range(4):
+        fill(T.br[:, k:k + 1], -2.0 ** (75 - k), "bn%d" % k)
+        B1.append("bn%d" % k)
+    ts(T.ip[:, 1:2], T.ip[:, 0:1], 15, A.bitwise_and, ["ip"], "ip1")
+    ts(T.ip[:, 2:3], T.ip[:, 0:1], 4, A.logical_shift_right, ["ip"], "ip2", 1, A.bitwise_and)
+    grow(neg, B1, "bn", [(4, 4, 4), (8, 4, 8), (12, 4, 12)])
+    grow(pos, B2, "bp", [(4, 4, 4), (8, 4, 8), (12, 4, 12)])
+    cp(cc(LANE), T.ip[:, 1:2], ["ip1"], "lane")
+    cp(cc(ODD), T.ip[:, 2:3], ["ip2"], "odd")
+    cp(T.opick[:, :], T.ipick[:, :], ["ipick"], "opick")
+    grow(neg, B1, "bn", [(16, 16, 16), (32, 16, 32), (48, 16, 48)])
+    grow(pos, B2, "bp", [(16, 16, 16), (32, 16, 32), (48, 16, 48)])
     lin(T.iw[:, 145:146], "iwc", LANE, 0.0, 2.0 ** 69)
     lin(T.wt[:, 145:146], "wtc", LANE, 0.0, 2.0 ** -69)
-    lin(T.nt1[:, 145:146], "ntc", LANE, 2.0 ** -73, -7 * 2.0 ** -73)
-    lin(cc(56), "cb", LANE, -0.9375, -0.9375)
-    lin(cc(E8), "e8", LANE, 0.125, -3.875)
-    lin(cc(L33), "l33", LANE, 33.0, 0.0)
-    lin(cc(O16), "o16", ODD, 16.0, 0.0)
-    lin(cc(L32), "l32", LANE, 32.0, 0.0)
-    act(T.nt1[:, 0:145], T.br[:, 1:146], AF.Identity, ["br", "cn"], ["nta"], scale=cc(CN))
-    act(T.nt1[:, 146:289], T.br[:, 146:289], AF.Identity, ["br2", "cp"], ["ntb"], scale=cc(CP))
-    act(T.sr1[:, :], T.su1[:, :].indirect(T.opick[:, :]), AF.Copy, ["qu1", "opick"], ["sr1"])
-    act(T.wt[:, 0:145], T.br[:, 1:146], AF.Identity, ["br"], ["wta"], scale=-1.0)
-    act(T.wt[:, 146:289], T.br[:, 146:289], AF.Identity, ["br2"], ["wtb"])
-    act(T.c[:, 40:44], T.br[:, 79:92:4], AF.Identity, ["br"], ["crow0"], scale=-1.0)
-    act(T.c[:, 44:46], T.br[:, 95:99:3], AF.Identity, ["br"], ["crow1"], scale=-1.0)
-    act(T.c[:, 48:53], T.br[:, 220:237:4], AF.Identity, ["br2"], ["drow0"])
-    act(T.c[:, 53:54], T.br[:, 239:240], AF.Identity, ["br2"], ["drow1"])
+    ts(T.otb[:, 6:7], cc(LANE), 17.0, A.mult, ["lane"], "otbd", 17.0, A.add)
+    ts(T.otb[:, 7:8], cc(LANE), 17.0, A.mult, ["lane"], "otbe", 17.0, A.add)
+    grow(neg, B1, "bn", [(64, 64, 64), (128, 18, 96)])
+    grow(pos, B2, "bp", [(64, 64, 64), (128, 16, 96)])
+    ts(T.otb[:, 0:4], T.itb[:, :], cc(LANE), A.add, ["itb", "lane"], "otba")
+    ts(T.otb[:, 4:5], cc(LANE), 216.0, A.add, ["lane"], "otbb")
+    ts(T.otb[:, 5:6], cc(LANE), 216.0, A.add, ["lane"], "otbc")
+    B = B1 + B2
+    quant("u1", 0, 128, T.tu1, ["tu1"], "qu1")
+    cp(T.tbr[:, 96:128], T.br[:, 0:290].indirect(T.otb[:, 6:8]), B + ["otbd", "otbe"], "tbr3")
+    cp(words(T.qr1[:, :]), words(T.qu1[:, :]).indirect(T.opick[:, :]), ["qu1", "opick"], "qr1")
+    turn(T.tbt[:, 96:128], T.tbr[:, 96:128], ["tbr3"], "tbt3")
+    FT = ["fta", "base"]
+    NT, WT, IW = ["nta", "ntb", "ntc"], ["wta", "wtb", "wtc"], ["iwa", "iwb", "iwc"]
 
-    for j in range(4):
-        quant("x", 128 * j, 128, T.tx, ["tx%d" % j], "qx%d" % j)
+    lin(cc(56), "cb", LANE, -0.9375, -0.9375)
+    lin(cc(CN), "cn", LANE, -0.0625, 1.9375)
+    lin(cc(CP), "cp", LANE, 0.0625, 1.0625)
+    lin(cc(LP1), "lp1", LANE, 1.0, 1.0)
+    lin(T.nt1[:, 145:146], "ntc", LANE, 2.0 ** -73, -7 * 2.0 ** -73)
+    act(T.sr1[:, :], T.su1[:, :].indirect(T.opick[:, :]), AF.Copy, ["qu1", "opick"], ["sr1"])
+    act(T.nt1[:, 0:145], T.br[:, 1:146], AF.Identity, B1 + ["cn"], ["nta"], scale=cc(CN))
+    act(T.nt1[:, 146:289], T.br[:, 146:289], AF.Identity, B2 + ["cp"], ["ntb"], scale=cc(CP))
+
+    def gap(k):
+        if k == 0:
+            act(T.wt[:, 0:145], T.br[:, 1:146], AF.Identity, B1, ["wta"], scale=-1.0)
+            act(T.wt[:, 146:289], T.br[:, 146:289], AF.Identity, B2, ["wtb"])
+            act(T.c[:, 40:44], T.br[:, 79:92:4], AF.Identity, B1, ["crow0"], scale=-1.0)
+            act(T.c[:, 44:46], T.br[:, 95:99:3], AF.Identity, B1, ["crow1"], scale=-1.0)
+        elif k == 1:
+            act(T.iw[:, 0:145], T.br[:, 142:287], AF.Identity, B, ["iwa"])
+            act(T.c[:, 48:53], T.br[:, 220:237:4], AF.Identity, B2, ["drow0"])
+            act(T.c[:, 53:54], T.br[:, 239:240], AF.Identity, B2, ["drow1"])
+        else:
+            lin(cc(E8), "e8", LANE, 0.125, -3.875)
+            lin(cc(L33), "l33", LANE, 33.0, 0.0)
+            lin(cc(L32), "l32", LANE, 32.0, 0.0)
+            lin(cc(O16), "o16", ODD, 16.0, 0.0)
+
+    quant("x", 0, 128, T.tx, ["tx0"], "qx0")
+    quant("x", 128, 128, T.tx, ["tx1"], "qx1")
+    ts(T.tb[:, 18:19], T.tbt[:, 96:97], -1.0, A.mult, ["tbt3"], "tbe")
+    ts(T.tb[:, 17:18], T.tbt[:, 96:97], 1.0, A.mult, ["tbt3"], "tbd")
+    quant("x", 256, 128, T.tx, ["tx2"], "qx2")
+    quant("x", 384, 128, T.tx, ["tx3"], "qx3")
+    cp(T.tbr[:, 0:96], T.br[:, 0:290].indirect(T.otb[:, 0:6]), B + ["otba", "otbb", "otbc"], "tbr")
+    fill(T.ft[:, 0:16], 0.0, "base")
+    ts(T.off[:, 1:2], cc(LANE), 0.0, A.is_equal, ["lane"], "off1", 8.0, A.mult)
+    turn(T.tbt[:, 0:96], T.tbr[:, 0:96], ["tbr"], "tbt")
+    fill(T.ges[:, :], 0.0, "ges0")
+    fill(T.zero[:, :], 0.0, "zero")
+    ts(T.tb[:, 0:8], T.br[:, 1:121:17], T.tbt[:, 0:1], A.mult, B1 + ["tbt"], "tba", -1.0, A.mult)
+    ts(T.tb[:, 9:17], T.br[:, 154:274:17], T.tbt[:, 64:65], A.mult, B2 + ["tbt"], "tbb")
+    ts(T.tb[:, 8:9], T.tbt[:, 32:33], 1.0, A.mult, ["tbt"], "tbc")
+    do("v", V.memset, T.ft[:, 1:2], 1.0, r=["base"], w=["fta"])
     R = ["qr1", "sr1"]
-    mm("p2", 384, "r1", 0, "x", 0, ["qx0", "qx1", "qx2"] + R)
-    mm("p3", 128, "r1", 0, "x", 384, ["qx3"] + R)
+    mm("p2", 256, "r1", 0, "x", 0, ["qx0", "qx1"] + R)
+    mm("p3", 256, "r1", 0, "x", 256, ["qx2", "qx3"] + R)
     for p in ("p0", "p1"):
         mm(p, 512, "r1", 0, "x", 0, ["qx%d" % j for j in range(4)] + R)
 
@@ -237,11 +261,14 @@ def rank_program(g, core, T, topo):
         if b == n:
             dma("s", ch[:, :], T.srow[0:128:16, 0:n], r=["srow0", "srow%d" % a], w=["ch"])
 
+    def base(t, h):
+        cp(T.xf[:, :].indirect(T.o1[:, 16 * t + 8 * h:16 * t + 8 * h + 8]), T.txh[:, 512 * h + t:512 * h + 512:4], ["o1_%d" % t, "txh", "xf0"], "xf")
+
     def jobs1():
         ts(cc(M8), cc(LANE), 8.0, A.is_lt, ["lane"], "m8")
+        yield
         ts(T.tr1[:, :], T.kr1[:, :], cc(L32), A.add, ["kr1", "l32"], "tr1")
         ts(cc(D6), cc(E8), cc(M8), A.mult, ["e8", "m8"], "d6", 4.0, A.add)
-        yield
         rows("p1", 512, T.ch1, 0, 256)
         yield
         rows("p1", 512, T.ch1, 256, 512)
@@ -252,34 +279,45 @@ def rank_program(g, core, T, topo):
         yield
         cp(words(T.qr2[:, :]), words(T.qu2[:, :]).indirect(T.opick[:, :]), ["qu2", "opick"], "qr2")
         yield
+        ts(T.ip[:, 5:6], T.ip[:, 1:2], 1, A.bitwise_and, ["ip1"], "ip5")
+        ts(cc(SO), cc(LANE), 16.0, A.mult, ["lane", "o16"], "so16", cc(O16), A.add)
         cp(T.sr2[:, :], T.su2[:, :].indirect(T.opick[:, :]), ["qu2", "opick"], "sr2")
         yield
-        fill(T.R1[:, 0:512], 0.0, "R1")
+        cp(cc(LB), T.ip[:, 5:6], ["ip5"], "lb")
+        fill(T.R1[:, 0:272], 0.0, "R1")
+        ts(T.sel1[:, 0:1], cc(LB), 240.0, A.mult, ["lb", "so16"], "sel1", cc(SO), A.add)
         yield
 
     def jobs2():
         ts(cc(L16), cc(LANE), 16.0, A.mult, ["lane"], "l16")
         ts(T.ip[:, 3:4], T.ip[:, 1:2], 2, A.logical_shift_right, ["ip1"], "ip3")
         ts(T.ip[:, 4:5], T.ip[:, 1:2], 3, A.bitwise_and, ["ip1"], "ip4")
+        ts(T.ip[:, 6:7], T.ip[:, 1:2], 7, A.bitwise_and, ["ip1"], "ip6")
         quant("E", 0, 128, T.te, ["te0"], "qE0", 0)
         yield
         quant("v", 0, 128, T.tv, ["tv"], "qvv")
         ts(T.tr2[:, :], T.kr2[:, :], cc(L16), A.add, ["kr2", "l16"], "tr2")
         cp(cc(LQ), T.ip[:, 3:4], ["ip3"], "lq")
         cp(cc(LR), T.ip[:, 4:5], ["ip4"], "lr")
+        cp(cc(L7), T.ip[:, 6:7], ["ip6"], "l7")
         yield
-        rows("p7", 256, T.ch2, 0, 256)
+        rows("p3", 256, T.ch2, 0, 256)
+        ts(cc(SO7), cc(L7), 16.0, A.mult, ["l7", "o16"], "so7", cc(O16), A.add)
+        ts(cc(LQ4), cc(ODD), -4.0, A.mult, ["odd", "lq"], "lq4", cc(LQ), A.add)
+        ts(cc(L4), cc(LR), 1024.0, A.add, ["lr"], "l4")
         yield
         quant("E", 128, 128, T.te, ["te1"], "qE1", 512)
-        yield
         quant("E", 256, 128, T.te, ["te2"], "qE2", 1024)
         yield
         quant("E", 384, 128, T.te, ["te3"], "qE3", 1536)
+        base(0, 0)
         yield
-        ts(cc(EVEN), cc(ODD), -1.0, A.mult, ["odd"], "even", 1.0, A.add)
-        ts(cc(L4), cc(LR), 1024.0, A.add, ["lr"], "l4")
-        ts(T.orep[:, :], T.irep[:, :], cc(LQ), A.add, ["irep", "lq"], "orep")
-        fill(T.R2[:, 0:256], 0.0, "R2")
+        ts(T.sel2[:, 0:1], cc(LB), 112.0, A.mult, ["lb", "so7"], "sel2", cc(SO7), A.add)
+        base(0, 1)
+        yield
+        fill(T.R2[:, 0:144], 0.0, "R2")
+        ts(T.orep[:, 0:33], T.irep[:, :], cc(LQ4), A.add, ["irep", "lq4"], "orep", 127.0, A.min)
+        ts(T.sel3[:, 0:1], cc(LB), 496.0, A.mult, ["lb", "so16"], "sel3a", cc(SO), A.add)
         yield
 
     def search(n, pa, pb, first, b, ch, jobs):
@@ -289,8 +327,8 @@ def rank_program(g, core, T, topo):
             for _ in jobs:
                 return
 
-        def count(t, j, tk, p, w, sign=-1.0):
-            act(T.sj[:, 0:w], T[p][:, 0:w], AF.Sign, [p, tk], ["sj", "sm%d" % j], scale=sign, bias=t, accum_out=sm(j))
+        def count(t, j, tk, p, w, sign=-1.0, buf="sj"):
+            act(T[buf][:, 0:w], T[p][:, 0:w], AF.Sign, [p, tk], [buf, "sm%d" % j], scale=sign, bias=t, accum_out=sm(j))
 
         def answer(j, n2=0):
             if n2:
@@ -299,22 +337,26 @@ def rank_program(g, core, T, topo):
                 ts(T.off[:, 0:1], sm(j), 0.0, A.is_le, ["sm%d" % j], "off0")
         if first:
             (p0, w0), (p1, w1) = first
-            count(T.tb[:, 18:19], 1, "tbe", p0, w0, 1.0)
+            count(T.tb[:, 18:19], 1, "tbe", p0, w0, 1.0, "sk")
             count(T.tb[:, 17:18], 0, "tbd", p1, w1)
-            cp(T.iw[:, 0:145], T.br[:, 142:287], B, "iwa")
-            ts(T.iw[:, 146:289], T.br[:, 5:148], -1.0, A.mult, B, "iwb")
+            gap(0)
         else:
             fill(sm(1), 0.0, "sm1")
             count(T.tb[:, 17:18], 0, "tbd", pa, n)
-        job()
+            job()
         ts(T.offb[:, 0:1], sm(0), sm(1), A.is_le, ["sm0", "sm1", "lp1"], "offb", cc(LP1), A.mult)
         cp(T.l64[:, 0:16], T.tb[:, 0:17].indirect(T.offb[:, 0:1]), ["offb", "tba", "tbb", "tbc"], "b16")
         cp(T.l64[:, 64:80], T.seq[:, 0:17].indirect(T.offb[:, 0:1]), ["offb", "seq"], "s16")
         red(sm(3), T.l64[:, 0:16], A.max, ["b16"], "sm3")
         red(sm(5), T.l64[:, 64:80], A.max, ["s16"], "sm5")
         count(sm(3), 4, "sm3", pa, n)
+        if first:
+            gap(1)
         ts(sm(2), cc(LP1), sm(5), A.add, ["lp1", "sm5"], "sm2")
         cp(T.offq[:, 1:2], sm(5), ["sm5"], "offq1")
+        if first:
+            ts(T.iw[:, 146:289], T.br[:, 5:148], -1.0, A.mult, B, "iwb")
+            job()
         ts(T.offq[:, 0:1], sm(4), 0.0, A.is_le, ["sm4", "sm2"], "offq0", sm(2), A.mult)
         answer(4)
         cp(T.l64[:, 96:128], T.nt1[:, 0:289].indirect(T.offq[:, 0:2]), ["offq0", "offq1"] + NT, "n32")
@@ -327,33 +369,35 @@ def rank_program(g, core, T, topo):
         for r in range(6):
             nx = "sm%d" % (16 + r)
 
-            def base():
+            def start():
                 ts(T.ft[:, 8:9], t, T.si8[:, r:r + 1], A.mult, [tk, "si8", ["cb", "cb5", "cb6"][max(r - 3, 0)]], "base", cc(56 if r < 4 else 56 + r), A.add)
             if r == 0:
                 count(t, 8, tk, pa, n)
+                if first:
+                    gap(2)
                 ts(T.si8[:, 0:6], T.c[:, 48:54], T.l64[:, 32:33], A.mult, ["i16", "drow0", "drow1"], "si8")
                 if n < 512:
                     answer(8)
                 ts(T.sc8[:, 0:6], T.c[:, 40:46], T.l64[:, 48:49], A.mult, ["w16", "crow0", "crow1"], "sc8")
-                base()
+                start()
                 if n == 512:
                     answer(8)
             elif r < 5:
                 count(t, 8 + r, tk, pa, n - b)
                 if b:
                     ts(T.sjv[:, 0:b], T[pb][:, n - b:n], t, A.is_ge, [pb, tk], "sjv0", 2.0, A.mult)
-                base()
+                start()
                 if b:
                     red(sm(14), T.sjv[:, 0:b], A.add, ["sjv0"], "sm14")
                 answer(8 + r, b)
             else:
                 m = n // 2
-                ts(T.sjv[:, 0:m], T[pb][:, 0:m], t, A.is_ge, [pb, tk], "sjv0")
-                ts(T.sjv[:, m:n], T[pb][:, m:n], t, A.is_ge, [pb, tk], "sjv1")
-                act(T.sj[:, 0:m], T.sjv[:, 0:m], AF.Copy, ["sjv0"], ["sj", "sm13"], accum_out=sm(13))
-                base()
-                red(sm(14), T.sjv[:, m:n], A.add, ["sjv1"], "sm14")
-                ts(T.off[:, 0:1], sm(14), sm(13), A.add, ["sm13", "sm14"], "off0", n / 2.0, A.is_ge)
+                ts(T.sjv[:, 0:m], T[pb][:, m:n], t, A.is_lt, [pb, tk], "sjv0")
+                act(T.sj[:, 0:m], T[pa][:, 0:m], AF.Sign, [pa, tk], ["sj"], scale=-1.0, bias=t)
+                start()
+                act(T.sk[:, 0:m], T.sj[:, 0:m], AF.Relu, ["sj"], ["sk", "sm13"], accum_out=sm(13))
+                red(sm(14), T.sjv[:, 0:m], A.add, ["sjv0"], "sm14")
+                ts(T.off[:, 0:1], sm(14), sm(13), A.add, ["sm13", "sm14"], "off0", n / 2.0, A.is_le)
             act(T.gj[:, 0:32], T.ft[:, :].indirect(T.off[:, 0:2]), AF.Identity, ["off0", "off1", "sc8"] + FT, ["gj", nx], scale=T.sc8[:, r:r + 1], accum_out=sm(16 + r))
             t, tk = sm(16 + r), nx
             job()
@@ -375,57 +419,73 @@ def rank_program(g, core, T, topo):
         ts(T.y1[:, 0:q], T.es2[:, 0:q], sm(32), A.add, ["es2", "sm32", "sm31"], "y1", sm(31), A.is_ge)
         tt(T.vi[:, 0:q], T.ges[:, 0:q], T.me[:, 0:q], A.add, ["gs", "ges0", "me"], "vi")
         tt(T.mm[:, 0:q], T.y1[:, 0:q], T.trn[:, 0:q], A.mult, ["y1", "trn"], "mm")
-        ts(T.vq[:, 0:q], T.vi[:, 0:q], 1008, A.bitwise_and, ["vi"], "vq")
-        tt(T.vg[:, 0:q], T.vi[:, 0:q], T.vq[:, 0:q], A.add, ["vi", "vq"], "vg")
-        tt(T.dd[:, 0:q], T.mm[:, 0:q], T.vg[:, 0:q], A.max, ["mm", "vg"], "dd")
-        so, R, rk, val, vk, Tr, W = (T.osc1, T.R1, "R1", T.val1, "val1", T.Tr1, T.W1) if n == 512 else (T.osc2, T.R2, "R2", T.val2, "val2", T.Tr2, T.W2)
+        tt(T.dd[:, 0:q], T.mm[:, 0:q], T.vi[:, 0:q], A.max, ["mm", "vi"], "dd")
+        so, R, rk, val, vk, Tr = (T.osc1, T.R1, "R1", T.val1, "val1", T.Tr1) if n == 512 else (T.osc2, T.R2, "R2", T.val2, "val2", T.Tr2)
         ts(so[:, :], T.dd[:, 0:q], cc(O16), A.add, ["dd", "o16"], "so")
         cp(R[:, :].indirect(so[:, :]), val[:, :], ["so", vk], rk)
-        do("v", V.transpose, Tr[:, :], R[:, 0:n], r=[rk], w=["Tr"])
-        tt(W[:, :], Tr[:, 0:n:32], Tr[:, 16:n:32], A.add, ["Tr"], "W%d" % n)
+        m = n // 2
+        turn(Tr[:, 0:m], R[:, 0:m], [rk], rk + "a")
+        turn(Tr[:, m:n], R[:, 16:m + 16], [rk], rk + "b")
 
-    def offsets(o, w, W, k, add):
-        for t in range(4):
-            ts(T[o][:, k * t:k * t + k], W[:, :], 4.0, A.mult, [w], "%s_%d" % (o, t), add + t, A.add)
+    L1T, L2T = ["R1a", "R1b", "sel1"], ["R2a", "R2b", "sel2"]
 
-    def gather(dst, m, src, rs, o, k, eng):
-        for t in range(4):
-            a = (T[dst][:, t:4 * m:4], src[:, :].indirect(T[o][:, k * t:k * t + k]))
-            r, w = rs + ["%s_%d" % (o, t)], "%s%d" % (dst, t)
-            if eng[t] == "a":
-                act(*a, AF.Copy, r, [w])
-            else:
-                cp(*a, r, w)
+    def pick(c, tr, sel, n, k, add, r, o, w):
+        ts(T[o][:, c:c + 16], T[tr][:, 0:n].indirect(T[sel][:, 0:1]), k, A.mult, r, w, add, A.add)
 
-    def layer(dst, q, b4, n, r):
-        for b in range(4):
-            p = "p%d" % (2 + b)
-            mm(p, n, q, 128 * b, b4, 0, r)
-            if b % 2 == 0:
-                act(T[dst][:, b:4 * n:4], T[p][:, 0:n], AF.Relu, [p], ["%s%d" % (dst, b)], scale=0.03125)
-            else:
-                ts(T[dst][:, b:4 * n:4], T[p][:, 0:n], 0.0, A.max, [p], "%s%d" % (dst, b), 0.03125, A.mult)
+    def gather(dst, h, t, src, rs, o, eng, w):
+        a = (T[dst][:, 512 * h + t:512 * h + 512:4], src[:, :].indirect(T[o][:, 16 * t + 8 * h:16 * t + 8 * h + 8]))
+        if eng == "a":
+            act(*a, AF.Copy, rs, [w])
+        else:
+            cp(*a, rs, w)
+
+    def relu(dst, h, b, p, eng, w):
+        o, i = T[dst][:, 512 * h + b:512 * h + 512:4], T[p][:, 0:128]
+        if eng == "a":
+            act(o, i, AF.Relu, [p], [w], scale=0.03125)
+        else:
+            ts(o, i, 0.0, A.max, [p], w, 0.03125, A.mult)
 
     def four(n):
         return ["%s%d" % (n, t) for t in range(4)]
 
-    search(512, "p0", "p1", (("p2", 384), ("p3", 128)), 64, T.ch1, jobs1())
+    search(512, "p0", "p1", (("p2", 256), ("p3", 256)), 64, T.ch1, jobs1())
     dma("s", T.tv[:, :], T.v[:, :], w=["tv"])
     dma("s", codes(T.qZ[:, :]), T.zc[:, :], w=["qZ"])
     dma("s", T.sZ[:, :], T.zs[:, :], w=["sZ"])
-    dma("s", T.xf[:, :], T.x[:, :], w=["xf"])
-    offsets("o1", "W512", T.W1, 16, 1024.0)
-    gather("tf", 256, T.tx, X, "o1", 16, "avav")
-    quant("F", 0, 256, T.tf, four("tf"), "qF")
-    layer("th", "W", "F", 256, ["qW", "sW", "qF"])
-    dma("s", T.txh[:, :], T.tf[:, :], r=four("tf"), w=["txh"])
-    dma("g", T.txh[:, :], T.th[:, :], r=four("th"), w=["txh"], accum_op=A.add)
-    quant("H", 0, 256, T.th, four("th"), "qH")
-    for p in ("p6", "p7"):
-        mm(p, 256, "r2", 0, "H", 0, ["qH", "qr2", "sr2"])
-    search(256, "p6", "p7", None, 0, T.ch2, jobs2())
-    offsets("o2", "W256", T.W2, 8, 0.0)
-    gather("tg", 128, T.th, four("th"), "o2", 8, "avav")
+    dma("s", T.xf[:, :], T.x[:, :], w=["xf0"])
+    for t in range(4):
+        pick(16 * t, "Tr1", "sel1", 512, 4.0, 1024.0 + t, L1T, "o1", "o1_%d" % t)
+    FA, FB, HA, HB = four("tfa"), four("tfb"), four("tha"), four("thb")
+    for t in range(4):
+        gather("tf", 0, t, T.tx, X + ["o1_%d" % t], "o1", "avav"[t], FA[t])
+    for t in range(3):
+        gather("tf", 1, t, T.tx, X + ["o1_%d" % t], "o1", "ava"[t], FB[t])
+    quant("F", 0, 128, T.tf, FA, "qFa")
+    gather("tf", 1, 3, T.tx, X + ["o1_3"], "o1", "v", FB[3])
+    quant("F", 128, 128, T.tf, FB, "qFb")
+    PA, PB = ["p2", "p3", "p4", "p5"], ["p6", "p7", "p0", "p1"]
+    for b in range(4):
+        mm(PA[b], 128, "W", 128 * b, "F", 0, ["qW", "sW", "qFa"])
+    for b in range(4):
+        mm(PB[b], 128, "W", 128 * b, "F", 128, ["qW", "sW", "qFb"])
+    for b in range(4):
+        relu("th", 0, b, PA[b], "avav"[b], HA[b])
+    relu("th", 1, 0, PB[0], "a", HB[0])
+    relu("th", 1, 1, PB[1], "v", HB[1])
+    quant("H", 0, 128, T.th, HA, "qHa")
+    relu("th", 1, 2, PB[2], "a", HB[2])
+    relu("th", 1, 3, PB[3], "v", HB[3])
+    quant("H", 128, 128, T.th, HB, "qHb")
+    dma("s", T.txh[:, :], T.tf[:, :], r=FA + FB, w=["txh"])
+    dma("g", T.txh[:, :], T.th[:, :], r=HA + HB, w=["txh"], accum_op=A.add)
+    for p in ("p2", "p3"):
+        mm(p, 256, "r2", 0, "H", 0, ["qHa", "qHb", "qr2", "sr2"])
+    search(256, "p2", "p3", None, 0, T.ch2, jobs2())
+    for t in range(4):
+        pick(16 * t, "Tr2", "sel2", 256, 4.0, float(t), L2T, "o2", "o2_%d" % t)
+    for t in range(4):
+        gather("tg", 0, t, T.th, HA + HB + ["o2_%d" % t], "o2", "avav"[t], "tg%d" % t)
     quant("G", 0, 128, T.tg, four("tg"), "qG")
 
     far = [d for d in range(N) if d != rank and topo.die(T.cores[d]) != topo.die(core)]
@@ -456,51 +516,49 @@ def rank_program(g, core, T, topo):
         wr[tok + "r"] = [("far", sem, total[sem], {})]
         total["sent"] = total.get("sent", 0) + 4 * (N - 1)
     swap("G", "L", "down")
-    ts(T.o1[:, 64:80], T.W1[:, :], 256.0, A.add, ["W512"], "o1c")
-    cp(T.o2[:, 32:40], T.W2[:, :], ["W256"], "o2c")
+    pick(64, "Tr1", "sel1", 512, 1.0, 256.0, L1T, "o1", "o1c")
+    pick(64, "Tr2", "sel2", 256, 1.0, 0.0, L2T, "o2", "o2c")
     act(T.L1r[:, :], T.ir[:, :].indirect(T.o1[:, 64:80]), AF.Identity, ["ir", "o1c"], ["L1r"])
-    act(T.olr[:, :], T.L1r[:, :].indirect(T.o2[:, 32:40]), AF.Identity, ["L1r", "o2c"], ["olr"])
+    act(T.olr[:, :], T.L1r[:, :].indirect(T.o2[:, 64:72]), AF.Identity, ["L1r", "o2c"], ["olr"])
     dma("s", T.ol[:, :], T.olr[0:128:16, :], r=["olr"], w=["ol"])
-    act(T.gap3[:, :], T.olr[:, :].indirect(T.orep[:, :]), AF.Identity, ["olr", "orep"], ["gap3"], bias=-256.0)
-
-    def base(t):
-        cp(T.xf[:, :].indirect(T.o1[:, 16 * t:16 * t + 16]), T.txh[:, t:1024:4], ["o1_%d" % t, "txh"], "xf")
-    base(0)
-    base(1)
-    layer("tt", "Z", "L", 128, ["qZ", "sZ", "qGo", "qGp", "qGr"])
+    act(T.gap3[:, :], T.olr[:, :].indirect(T.orep[:, 0:33]), AF.Identity, ["olr", "orep"], ["gap3"], bias=-256.0)
+    ts(T.sel3[:, 1:2], T.sel3[:, 0:1], 256.0, A.add, ["sel3a"], "sel3b")
+    for t, h in ((1, 0), (1, 1), (2, 0)):
+        base(t, h)
+    for b in range(4):
+        mm(PA[b], 128, "Z", 128 * b, "L", 0, ["qZ", "sZ", "qGo", "qGp", "qGr"])
+    for b in range(4):
+        relu("tt", 0, b, PA[b], "avav"[b], "tt%d" % b)
     quant("T", 0, 128, T.tt, four("tt"), "qT")
     swap("T", "U", "up")
-    do("v", V.transpose, T.Tr3[:, :], T.gap3[:, :], r=["gap3"], w=["Tr3"])
-    ts(T.W3[:, 0:32], T.Tr3[:, 0:1024:32], cc(EVEN), A.mult, ["Tr3", "even"], "w3a")
-    ts(T.W3[:, 32:64], T.Tr3[:, 16:1024:32], cc(ODD), A.mult, ["Tr3", "odd"], "w3b")
-    tt(T.W3[:, 64:96], T.W3[:, 0:32], T.W3[:, 32:64], A.add, ["w3a", "w3b"], "w3c")
-    ts(T.o3[:, :], T.W3[:, 64:96], 4.0, A.mult, ["w3c", "l4"], "o3", cc(L4), A.add)
+    turn(T.Tr3[:, 0:512], T.gap3[:, 0:512], ["gap3"], "Tr3a")
+    turn(T.Tr3[:, 512:1024], T.gap3[:, 16:528], ["gap3"], "Tr3b")
+    ts(T.o3[:, :], T.Tr3[:, :].indirect(T.sel3[:, 0:2]), 4.0, A.mult, ["Tr3a", "Tr3b", "sel3a", "sel3b", "l4"], "o3", cc(L4), A.add)
     act(T.txg[:, :], T.tx[:, :].indirect(T.o3[:, :]), AF.Copy, X + ["o3"], ["txg"])
-    base(2)
-    base(3)
+    for t, h in ((2, 1), (3, 0), (3, 1)):
+        base(t, h)
     for b in range(4):
-        mm("p%d" % (2 + b), 128, "E", 128 * b, "U", 0, ["qE%d" % b, "qTo", "qTp", "qTr"])
+        mm(PA[b], 128, "E", 128 * b, "U", 0, ["qE%d" % b, "qTo", "qTp", "qTr"])
     for b in range(4):
-        tt(T.thn[:, b:512:4], T["p%d" % (2 + b)][:, 0:128], T.tg[:, b:512:4], A.add, ["p%d" % (2 + b), "tg%d" % b], "thn%d" % b)
+        tt(T.thn[:, b:512:4], T[PA[b]][:, 0:128], T.tg[:, b:512:4], A.add, [PA[b], "tg%d" % b], "thn%d" % b)
     for b in range(4):
         tt(T.txn[:, b:512:4], T.txg[:, b:512:4], T.thn[:, b:512:4], A.add, ["txg", "thn%d" % b], "txn%d" % b)
     cp(T.xf[:, :].indirect(T.o3[:, :]), T.txn[:, :], ["o3"] + four("txn"), "xf")
-    for h, (c, n) in enumerate(((0, 256), (256, 128), (384, 128))):
-        p = "p%d" % h
-        quant("N", c, n, T.xf, ["xf"], "qN%d" % h)
-        mm(p, n, "v", 0, "N", c, ["qvv", "qN%d" % h])
-    for h, (c, n) in enumerate(((0, 256), (256, 128), (384, 128))):
-        o, i = T.ysb[:, c:c + n], T["p%d" % h][:, 0:n]
-        if h < 1:
-            act(o, i, AF.Copy, ["p%d" % h], ["y%d" % h])
+    for h in range(4):
+        quant("N", 128 * h, 128, T.xf, ["xf"], "qN%d" % h)
+        mm(PB[h], 128, "v", 0, "N", 128 * h, ["qvv", "qN%d" % h])
+    for h in range(4):
+        o, i = T.ysb[:, 128 * h:128 * h + 128], T[PB[h]][:, 0:128]
+        if h % 2 == 0:
+            act(o, i, AF.Copy, [PB[h]], ["y%d" % h])
         else:
-            cp(o, i, ["p%d" % h], "y%d" % h)
-    dma("s", T.oc[:, 0:1024], codes(T.qN[:, 0:256]), r=["qN0"], w=["oc0"])
-    dma("s", T.oc[:, 1024:2048], codes(T.qN[:, 256:512]), r=["qN1", "qN2"], w=["oc1"])
+            cp(o, i, [PB[h]], "y%d" % h)
+    dma("s", T.oc[:, 0:1024], codes(T.qN[:, 0:256]), r=["qN0", "qN1"], w=["oc0"])
+    dma("s", T.oc[:, 1024:2048], codes(T.qN[:, 256:512]), r=["qN2", "qN3"], w=["oc1"])
     for j in range(4):
-        dma("s", T.osc[4 * j:4 * j + 4, :], T.sN[32 * j:32 * j + 4, :], r=["qN0", "qN1", "qN2"], w=["osc%d" % j])
-    dma("s", T.y[:, 0:256], T.ysb[:, 0:256], r=["y0"], w=["yo0"])
-    dma("a", T.y[:, 256:512], T.ysb[:, 256:512], r=["y1", "y2"], w=["yo1"])
+        dma("s", T.osc[4 * j:4 * j + 4, :], T.sN[32 * j:32 * j + 4, :], r=["qN%d" % h for h in range(4)], w=["osc%d" % j])
+    dma("a", T.y[:, 0:256], T.ysb[:, 0:256], r=["y0", "y1"], w=["yo0"])
+    dma("s", T.y[:, 256:512], T.ysb[:, 256:512], r=["y2", "y3"], w=["yo1"])
     for s in sorted(total):
         if seen.get(s, 0) < total[s]:
             g.wait_ge(T.sem[s], total[s])

from concourse.bass import DstId, RemoteDMATransfer
from concourse.mybir import dt, AluOpType as A, AxisListType, ActivationFunctionType as AF

F8, U8, BF, F32, I32, U16 = "float8_e4m3fn_x4", "uint8", "bfloat16", "float32", "int32", "uint16"
SCRATCH = {}
for _d, _l in (
    (BF, "tu1 512 tu2 512 tv 512 tx 2048 xf 2048 tf 1024 th 1024 txh 1024 tg 512 tt 512 thn 512 txg 512 txn 512 ones 512 te 2048 "
         "tot 528 ps 1056 val1 512 val2 256 sj 512 sk 512 sjv 512 R1 1056 R2 544 Tr1 512 Tr2 256 Tr3 1024 gap3 528"),
    (F32, "br 296 wt 296 iw 296 nt1 296 tbr 128 tbt 128 tb 24 seq 24 ft 16 ir 512 kr1 32 kr2 16 tr1 32 tr2 16 zero 32 c 64 gj 64 l64 128 "
          "sc8 8 si8 8 sm 64 srow 512 ch1 32 ch2 16 gt 32 eq 32 lt 32 ges 72 es2 32 ngt 32 trn 32 y1 32 me 32 dd 32 mm 32 vi 32 "
          "L1r 256 olr 128 ysb 512"),
    (I32, "ip 8 ipick 8 itb 4 irep 33"),
    (U16, "opick 8 otb 8 orep 34 off 2 offb 2 offn 2 offq 2 og 2 osc1 32 osc2 16 o1 80 o2 80 o3 32 sel1 2 sel2 2 sel3 2")):
    _l = _l.split()
    for _i in range(0, len(_l), 2):
        SCRATCH[_l[_i]] = ("sbuf", [128, int(_l[_i + 1])], _d)
for _n, _w in (("W", 512), ("Z", 512), ("x", 512), ("N", 512), ("E", 512), ("F", 256), ("H", 256), ("u1", 128), ("u2", 128), ("r1", 128), ("r2", 128), ("v", 128),
               ("G", 128), ("L", 128), ("T", 128), ("U", 128)):
    SCRATCH["q" + _n] = ("sbuf", [128, _w], F8)
    SCRATCH["s" + _n] = ("sbuf", [128, _w], U8)
for _i in range(8):
    SCRATCH["p%d" % _i] = ("psum", [128, 512], F32)
SEMAPHORES = ["qv", "qa", "qt", "qg", "down", "up", "sent"] + ["d%d" % i for i in range(44)]


def rank_program(g, core, T, topo):
    rank = T.rank_of(core)
    if rank is None:
        return
    N = len(T.cores)
    V, S, P = g.vector, g.scalar, g.tensor
    ENG = {"v": V, "a": S, "t": P, "g": g, "s": g.sync}
    clock = {q: {} for q in ENG}
    total, seen, wr, rd, nd = {}, {}, {}, {}, [0]

    def learn(q, deps):
        want = {}
        for _, s, n, _c in deps:
            want[s] = max(want.get(s, 0), n)
        for s in sorted(want):
            n = want[s]
            if clock[q].get(s, 0) >= n:
                continue
            if any(d[1] != s and want[d[1]] == d[2] and d[3].get(s, 0) >= n for d in deps if clock[q].get(d[1], 0) < d[2]):
                continue
            ENG[q].wait_ge(T.sem[s], n)
            seen[s] = max(seen.get(s, 0), n)
        for d in deps:
            for s, n in list(d[3].items()) + [(d[1], d[2])]:
                clock[q][s] = max(clock[q].get(s, 0), n)

    def deps_of(r, w):
        deps = []
        for t in r:
            deps += wr.get(t, [])
        for t in w:
            deps += wr.get(t, []) + rd.get(t, [])
        return deps

    def note(q, s, n, r, w, base):
        e = (q, s, n, dict(base))
        for t in w:
            wr[t], rd[t] = [e], []
        for t in r:
            if t not in w:
                rd.setdefault(t, []).append(e)

    def do(q, fn, *a, r=(), w=(), **k):
        learn(q, deps_of(r, w))
        s = "q" + q
        total[s] = total.get(s, 0) + 1
        fn(*a, **k).then_inc(T.sem[s], 1)
        note(q, s, total[s], r, w, clock[q])

    def dma(q, out, in_, r=(), w=(), **k):
        learn(q, deps_of(r, w))
        s = "d%d" % nd[0]
        nd[0] += 1
        total[s] = 16
        ENG[q].dma_start(out, in_, **k).then_inc(T.sem[s], 16)
        note(q, s, 16, r, w, clock[q])

    def mm(p, n, a, ac, b, bc, r):
        do("t", P.matmul_mx, T[p][:, 0:n], T["q" + a][:, ac:ac + 128], T["s" + a][:, ac:ac + 128], T["q" + b][:, bc:bc + n], T["s" + b][:, bc:bc + n], True, True, r=r, w=[p])

    def quant(q, c, n, t, r, w, tc=None):
        tc = 4 * c if tc is None else tc
        do("v", V.quantize_mx, T["q" + q][:, c:c + n], T["s" + q][:, c:c + n], t[:, tc:tc + 4 * n], r=r, w=[w])

    def ts(out, in0, s1, op0, r, w, s2=None, op1=None):
        do("v", V.tensor_scalar, out, in0, s1, s2, op0, *([] if op1 is None else [op1]), r=r, w=[w])

    def tt(out, a, b, op, r, w):
        do("v", V.tensor_tensor, out, a, b, op, r=r, w=[w])

    def red(out, in_, op, r, w):
        do("v", V.tensor_reduce, out, in_, AxisListType.X, op, r=r, w=[w])

    def scan(out, a, z, r, w):
        do("v", V.tensor_tensor_scan, out, a, z, 0.0, A.add, A.add, r=r, w=[w])

    def turn(out, in_, r, w):
        do("v", V.transpose, out, in_, r=r, w=[w])

    def fill(ap, x, w):
        do("v", V.memset, ap, x, w=[w])

    def cp(out, in_, r, w):
        do("v", V.tensor_copy, out, in_, r=r, w=[w])

    def act(out, in_, f, r, w, **k):
        do("a", S.activation, out, in_, f, r=r, w=w, **k)

    def codes(v):
        return v.bitcast(dt.uint8)

    def words(v):
        return v.bitcast(dt.uint32)

    def cc(j):
        return T.c[:, j:j + 1]

    def sm(j):
        return T.sm[:, j:j + 1]

    dma("s", T.tu1[:, :], T.u1[:, :], w=["tu1"])
    for j in range(4):
        dma("a" if j % 2 == 0 else "s", T.tx[:, 512 * j:512 * j + 512], T.x[:, 512 * j:512 * j + 512], w=["tx%d" % j])
    X = ["tx%d" % j for j in range(4)]

    def iota(n, pattern, base, cm=0):
        k = 1
        for _s, m in pattern:
            k *= m
        f = {} if SCRATCH[n][2] == I32 else {"allow_small_or_imprecise_dtypes": True}
        do("g", g.iota, T[n][:, 0:k], pattern, base, cm, w=[n], **f)

    def select(out, src, pattern, op, base, cm, r, w):
        do("g", g.affine_select, out, src, pattern, op, 0.0, base, cm, r=r, w=[w])
    iota("ip", [[1, 1]], 0, 1)
    iota("itb", [[62, 2], [0, 2]], 75)
    iota("ipick", [[16, 8]], 0)
    iota("seq", [[17, 17]], 0)
    iota("kr1", [[1, 32]], 512)
    iota("tot", [[0, 16], [1, 33]], 0)
    select(T.ps[0:16, 0:528], T.tot[0:16, :], [[-1, 16], [0, 33]], A.is_gt, 0, 1, ["tot"], "psa")
    select(T.ps[0:16, 528:1056], T.tot[0:16, :], [[1, 16], [0, 33]], A.is_ge, 0, -1, ["tot"], "psb")
    iota("val1", [[1, 32], [32, 16]], -256)
    iota("kr2", [[1, 16]], 256)
    iota("val2", [[1, 16], [16, 16]], 0)
    iota("irep", [[4, 33]], 0)
    iota("ir", [[1, 512]], 0)
    iota("ones", [[0, 512]], 1)
    for b in range(4):
        select(T.te[:, 512 * b:512 * b + 512], T.ones[:, :], [[1, 512]], A.is_equal, -b, -4, ["ones"], "te%d" % b)
    LANE, ODD, LP1, CN, CP, L33, O16, EVEN, L32, M8, E8, D6, L16, LQ, LR, L4, LB, SO, SO7, L7, LQ4 = range(21)
    B1, B2 = [], []

    def lin(out, w, src, k, add):
        act(out, cc(src), AF.Identity, ["lane", "odd"], [w], scale=k, bias=add)

    def neg(k, n, s):
        ts(T.br[:, k:k + n], T.br[:, k - s:k - s + n], 2.0 ** -s, A.mult, list(B1), "bn%d" % k)

    def pos(k, n, s):
        act(T.br[:, 146 + k:146 + k + n], T.br[:, 146 + k - s:146 + k - s + n], AF.Identity, list(B2), ["bp%d" % k], scale=2.0 ** s)

    def grow(f, B, n, parts):
        for p in parts:
            f(*p)
        B += [n + "%d" % p[0] for p in parts]
    for k in range(4):
        fill(T.br[:, 146 + k:147 + k], 2.0 ** (k - 70), "bp%d" % k)
        B2.append("bp%d" % k)
    for k in range(4):
        fill(T.br[:, k:k + 1], -2.0 ** (75 - k), "bn%d" % k)
        B1.append("bn%d" % k)
    ts(T.ip[:, 1:2], T.ip[:, 0:1], 15, A.bitwise_and, ["ip"], "ip1")
    ts(T.ip[:, 2:3], T.ip[:, 0:1], 4, A.logical_shift_right, ["ip"], "ip2", 1, A.bitwise_and)
    grow(neg, B1, "bn", [(4, 4, 4), (8, 4, 8), (12, 4, 12)])
    grow(pos, B2, "bp", [(4, 4, 4), (8, 4, 8), (12, 4, 12)])
    cp(cc(LANE), T.ip[:, 1:2], ["ip1"], "lane")
    cp(cc(ODD), T.ip[:, 2:3], ["ip2"], "odd")
    cp(T.opick[:, :], T.ipick[:, :], ["ipick"], "opick")
    grow(neg, B1, "bn", [(16, 16, 16), (32, 16, 32), (48, 16, 48)])
    grow(pos, B2, "bp", [(16, 16, 16), (32, 16, 32), (48, 16, 48)])
    lin(T.iw[:, 145:146], "iwc", LANE, 0.0, 2.0 ** 69)
    lin(T.wt[:, 145:146], "wtc", LANE, 0.0, 2.0 ** -69)
    ts(T.otb[:, 6:7], cc(LANE), 17.0, A.mult, ["lane"], "otbd", 17.0, A.add)
    ts(T.otb[:, 7:8], cc(LANE), 17.0, A.mult, ["lane"], "otbe", 17.0, A.add)
    grow(neg, B1, "bn", [(64, 64, 64), (128, 18, 96)])
    grow(pos, B2, "bp", [(64, 64, 64), (128, 16, 96)])
    ts(T.otb[:, 0:4], T.itb[:, :], cc(LANE), A.add, ["itb", "lane"], "otba")
    ts(T.otb[:, 4:5], cc(LANE), 216.0, A.add, ["lane"], "otbb")
    ts(T.otb[:, 5:6], cc(LANE), 216.0, A.add, ["lane"], "otbc")
    B = B1 + B2
    quant("u1", 0, 128, T.tu1, ["tu1"], "qu1")
    cp(T.tbr[:, 96:128], T.br[:, 0:290].indirect(T.otb[:, 6:8]), B + ["otbd", "otbe"], "tbr3")
    cp(words(T.qr1[:, :]), words(T.qu1[:, :]).indirect(T.opick[:, :]), ["qu1", "opick"], "qr1")
    turn(T.tbt[:, 96:128], T.tbr[:, 96:128], ["tbr3"], "tbt3")
    FT = ["fta", "base"]
    NT, WT, IW = ["nta", "ntb", "ntc"], ["wta", "wtb", "wtc"], ["iwa", "iwb", "iwc"]

    lin(cc(56), "cb", LANE, -0.9375, -0.9375)
    lin(cc(CN), "cn", LANE, -0.0625, 1.9375)
    lin(cc(CP), "cp", LANE, 0.0625, 1.0625)
    lin(cc(LP1), "lp1", LANE, 1.0, 1.0)
    lin(T.nt1[:, 145:146], "ntc", LANE, 2.0 ** -73, -7 * 2.0 ** -73)
    act(T.sr1[:, :], T.su1[:, :].indirect(T.opick[:, :]), AF.Copy, ["qu1", "opick"], ["sr1"])
    act(T.nt1[:, 0:145], T.br[:, 1:146], AF.Identity, B1 + ["cn"], ["nta"], scale=cc(CN))
    act(T.nt1[:, 146:289], T.br[:, 146:289], AF.Identity, B2 + ["cp"], ["ntb"], scale=cc(CP))

    def gap(k):
        if k == 0:
            act(T.wt[:, 0:145], T.br[:, 1:146], AF.Identity, B1, ["wta"], scale=-1.0)
            act(T.wt[:, 146:289], T.br[:, 146:289], AF.Identity, B2, ["wtb"])
            act(T.c[:, 40:44], T.br[:, 79:92:4], AF.Identity, B1, ["crow0"], scale=-1.0)
            act(T.c[:, 44:46], T.br[:, 95:99:3], AF.Identity, B1, ["crow1"], scale=-1.0)
        elif k == 1:
            act(T.iw[:, 0:145], T.br[:, 142:287], AF.Identity, B, ["iwa"])
            act(T.c[:, 48:53], T.br[:, 220:237:4], AF.Identity, B2, ["drow0"])
            act(T.c[:, 53:54], T.br[:, 239:240], AF.Identity, B2, ["drow1"])
        else:
            lin(cc(E8), "e8", LANE, 0.125, -3.875)
            lin(cc(L33), "l33", LANE, 33.0, 0.0)
            lin(cc(L32), "l32", LANE, 32.0, 0.0)
            lin(cc(O16), "o16", ODD, 16.0, 0.0)

    quant("x", 0, 128, T.tx, ["tx0"], "qx0")
    quant("x", 128, 128, T.tx, ["tx1"], "qx1")
    ts(T.tb[:, 18:19], T.tbt[:, 96:97], -1.0, A.mult, ["tbt3"], "tbe")
    ts(T.tb[:, 17:18], T.tbt[:, 96:97], 1.0, A.mult, ["tbt3"], "tbd")
    quant("x", 256, 128, T.tx, ["tx2"], "qx2")
    quant("x", 384, 128, T.tx, ["tx3"], "qx3")
    cp(T.tbr[:, 0:96], T.br[:, 0:290].indirect(T.otb[:, 0:6]), B + ["otba", "otbb", "otbc"], "tbr")
    fill(T.ft[:, 0:16], 0.0, "base")
    ts(T.off[:, 1:2], cc(LANE), 0.0, A.is_equal, ["lane"], "off1", 8.0, A.mult)
    turn(T.tbt[:, 0:96], T.tbr[:, 0:96], ["tbr"], "tbt")
    fill(T.ges[:, :], 0.0, "ges0")
    fill(T.zero[:, :], 0.0, "zero")
    ts(T.tb[:, 0:8], T.br[:, 1:121:17], T.tbt[:, 0:1], A.mult, B1 + ["tbt"], "tba", -1.0, A.mult)
    ts(T.tb[:, 9:17], T.br[:, 154:274:17], T.tbt[:, 64:65], A.mult, B2 + ["tbt"], "tbb")
    ts(T.tb[:, 8:9], T.tbt[:, 32:33], 1.0, A.mult, ["tbt"], "tbc")
    do("v", V.memset, T.ft[:, 1:2], 1.0, r=["base"], w=["fta"])
    R = ["qr1", "sr1"]
    mm("p2", 256, "r1", 0, "x", 0, ["qx0", "qx1"] + R)
    mm("p3", 256, "r1", 0, "x", 256, ["qx2", "qx3"] + R)
    for p in ("p0", "p1"):
        mm(p, 512, "r1", 0, "x", 0, ["qx%d" % j for j in range(4)] + R)

    learn("s", [d for t in X for d in wr[t]])
    dma("s", T.tu2[:, :], T.u2[:, :], w=["tu2"])
    dma("s", codes(T.qW[:, :]), T.wc[:, :], w=["qW"])
    dma("s", T.sW[:, :], T.ws[:, :], w=["sW"])
    for j in range(1, 8):
        dma("s", T.ps[16 * j:16 * j + 16, :], T.ps[0:16, :], r=["psa", "psb"], w=["ps%d" % j])
    PS = ["psa", "psb"] + ["ps%d" % j for j in range(1, 8)]

    def rows(pb, n, ch, a, b):
        cp(T.srow[:, a:b], T[pb][:, a:b], [pb], "srow%d" % a)
        if b == n:
            dma("s", ch[:, :], T.srow[0:128:16, 0:n], r=["srow0", "srow%d" % a], w=["ch"])

    def base(t, h):
        cp(T.xf[:, :].indirect(T.o1[:, 16 * t + 8 * h:16 * t + 8 * h + 8]), T.txh[:, 512 * h + t:512 * h + 512:4], ["o1_%d" % t, "txh", "xf0"], "xf")

    def jobs1():
        ts(cc(M8), cc(LANE), 8.0, A.is_lt, ["lane"], "m8")
        yield
        ts(T.tr1[:, :], T.kr1[:, :], cc(L32), A.add, ["kr1", "l32"], "tr1")
        ts(cc(D6), cc(E8), cc(M8), A.mult, ["e8", "m8"], "d6", 4.0, A.add)
        rows("p1", 512, T.ch1, 0, 256)
        yield
        rows("p1", 512, T.ch1, 256, 512)
        yield
        ts(cc(60), cc(D6), cc(LP1), A.subtract, ["d6", "lp1"], "cb5")
        ts(cc(61), cc(D6), -8.0, A.mult, ["d6"], "cb6")
        quant("u2", 0, 128, T.tu2, ["tu2"], "qu2")
        yield
        cp(words(T.qr2[:, :]), words(T.qu2[:, :]).indirect(T.opick[:, :]), ["qu2", "opick"], "qr2")
        yield
        ts(T.ip[:, 5:6], T.ip[:, 1:2], 1, A.bitwise_and, ["ip1"], "ip5")
        ts(cc(SO), cc(LANE), 16.0, A.mult, ["lane", "o16"], "so16", cc(O16), A.add)
        cp(T.sr2[:, :], T.su2[:, :].indirect(T.opick[:, :]), ["qu2", "opick"], "sr2")
        yield
        cp(cc(LB), T.ip[:, 5:6], ["ip5"], "lb")
        fill(T.R1[:, 0:272], 0.0, "R1")
        ts(T.sel1[:, 0:1], cc(LB), 240.0, A.mult, ["lb", "so16"], "sel1", cc(SO), A.add)
        yield

    def jobs2():
        ts(cc(L16), cc(LANE), 16.0, A.mult, ["lane"], "l16")
        ts(T.ip[:, 3:4], T.ip[:, 1:2], 2, A.logical_shift_right, ["ip1"], "ip3")
        ts(T.ip[:, 4:5], T.ip[:, 1:2], 3, A.bitwise_and, ["ip1"], "ip4")
        ts(T.ip[:, 6:7], T.ip[:, 1:2], 7, A.bitwise_and, ["ip1"], "ip6")
        quant("E", 0, 128, T.te, ["te0"], "qE0", 0)
        yield
        quant("v", 0, 128, T.tv, ["tv"], "qvv")
        ts(T.tr2[:, :], T.kr2[:, :], cc(L16), A.add, ["kr2", "l16"], "tr2")
        cp(cc(LQ), T.ip[:, 3:4], ["ip3"], "lq")
        cp(cc(LR), T.ip[:, 4:5], ["ip4"], "lr")
        cp(cc(L7), T.ip[:, 6:7], ["ip6"], "l7")
        yield
        rows("p3", 256, T.ch2, 0, 256)
        ts(cc(SO7), cc(L7), 16.0, A.mult, ["l7", "o16"], "so7", cc(O16), A.add)
        ts(cc(LQ4), cc(ODD), -4.0, A.mult, ["odd", "lq"], "lq4", cc(LQ), A.add)
        ts(cc(L4), cc(LR), 1024.0, A.add, ["lr"], "l4")
        yield
        quant("E", 128, 128, T.te, ["te1"], "qE1", 512)
        quant("E", 256, 128, T.te, ["te2"], "qE2", 1024)
        yield
        quant("E", 384, 128, T.te, ["te3"], "qE3", 1536)
        base(0, 0)
        yield
        ts(T.sel2[:, 0:1], cc(LB), 112.0, A.mult, ["lb", "so7"], "sel2", cc(SO7), A.add)
        base(0, 1)
        yield
        fill(T.R2[:, 0:144], 0.0, "R2")
        ts(T.orep[:, 0:33], T.irep[:, :], cc(LQ4), A.add, ["irep", "lq4"], "orep", 127.0, A.min)
        ts(T.sel3[:, 0:1], cc(LB), 496.0, A.mult, ["lb", "so16"], "sel3a", cc(SO), A.add)
        yield

    def search(n, pa, pb, first, b, ch, jobs):
        q = n // 16

        def job():
            for _ in jobs:
                return

        def count(t, j, tk, p, w, sign=-1.0, buf="sj"):
            act(T[buf][:, 0:w], T[p][:, 0:w], AF.Sign, [p, tk], [buf, "sm%d" % j], scale=sign, bias=t, accum_out=sm(j))

        def answer(j, n2=0):
            if n2:
                ts(T.off[:, 0:1], sm(14), sm(j), A.subtract, ["sm14", "sm%d" % j], "off0", float(n2), A.is_ge)
            else:
                ts(T.off[:, 0:1], sm(j), 0.0, A.is_le, ["sm%d" % j], "off0")
        if first:
            (p0, w0), (p1, w1) = first
            count(T.tb[:, 18:19], 1, "tbe", p0, w0, 1.0, "sk")
            count(T.tb[:, 17:18], 0, "tbd", p1, w1)
            gap(0)
        else:
            fill(sm(1), 0.0, "sm1")
            count(T.tb[:, 17:18], 0, "tbd", pa, n)
            job()
        ts(T.offb[:, 0:1], sm(0), sm(1), A.is_le, ["sm0", "sm1", "lp1"], "offb", cc(LP1), A.mult)
        cp(T.l64[:, 0:16], T.tb[:, 0:17].indirect(T.offb[:, 0:1]), ["offb", "tba", "tbb", "tbc"], "b16")
        cp(T.l64[:, 64:80], T.seq[:, 0:17].indirect(T.offb[:, 0:1]), ["offb", "seq"], "s16")
        red(sm(3), T.l64[:, 0:16], A.max, ["b16"], "sm3")
        red(sm(5), T.l64[:, 64:80], A.max, ["s16"], "sm5")
        count(sm(3), 4, "sm3", pa, n)
        if first:
            gap(1)
        ts(sm(2), cc(LP1), sm(5), A.add, ["lp1", "sm5"], "sm2")
        cp(T.offq[:, 1:2], sm(5), ["sm5"], "offq1")
        if first:
            ts(T.iw[:, 146:289], T.br[:, 5:148], -1.0, A.mult, B, "iwb")
            job()
        ts(T.offq[:, 0:1], sm(4), 0.0, A.is_le, ["sm4", "sm2"], "offq0", sm(2), A.mult)
        answer(4)
        cp(T.l64[:, 96:128], T.nt1[:, 0:289].indirect(T.offq[:, 0:2]), ["offq0", "offq1"] + NT, "n32")
        act(T.gj[:, 0:16], T.ft[:, 0:8].indirect(T.off[:, 0:1]), AF.Identity, ["off0"] + FT, ["gj", "sm6"], accum_out=sm(6))
        red(sm(7), T.l64[:, 96:128], A.max, ["n32"], "sm7")
        ts(T.offn[:, 0:1], sm(6), sm(5), A.add, ["sm6", "sm5"], "offn")
        cp(T.l64[:, 32:48], T.iw[:, 0:289].indirect(T.offn[:, 0:1]), ["offn"] + IW, "i16")
        cp(T.l64[:, 48:64], T.wt[:, 0:289].indirect(T.offn[:, 0:1]), ["offn"] + WT, "w16")
        t, tk = sm(7), "sm7"
        for r in range(6):
            nx = "sm%d" % (16 + r)

            def start():
                ts(T.ft[:, 8:9], t, T.si8[:, r:r + 1], A.mult, [tk, "si8", ["cb", "cb5", "cb6"][max(r - 3, 0)]], "base", cc(56 if r < 4 else 56 + r), A.add)
            if r == 0:
                count(t, 8, tk, pa, n)
                if first:
                    gap(2)
                ts(T.si8[:, 0:6], T.c[:, 48:54], T.l64[:, 32:33], A.mult, ["i16", "drow0", "drow1"], "si8")
                if n < 512:
                    answer(8)
                ts(T.sc8[:, 0:6], T.c[:, 40:46], T.l64[:, 48:49], A.mult, ["w16", "crow0", "crow1"], "sc8")
                start()
                if n == 512:
                    answer(8)
            elif r < 5:
                count(t, 8 + r, tk, pa, n - b)
                if b:
                    ts(T.sjv[:, 0:b], T[pb][:, n - b:n], t, A.is_ge, [pb, tk], "sjv0", 2.0, A.mult)
                start()
                if b:
                    red(sm(14), T.sjv[:, 0:b], A.add, ["sjv0"], "sm14")
                answer(8 + r, b)
            else:
                m = n // 2
                ts(T.sjv[:, 0:m], T[pb][:, m:n], t, A.is_lt, [pb, tk], "sjv0")
                act(T.sj[:, 0:m], T[pa][:, 0:m], AF.Sign, [pa, tk], ["sj"], scale=-1.0, bias=t)
                start()
                act(T.sk[:, 0:m], T.sj[:, 0:m], AF.Relu, ["sj"], ["sk", "sm13"], accum_out=sm(13))
                red(sm(14), T.sjv[:, 0:m], A.add, ["sjv0"], "sm14")
                ts(T.off[:, 0:1], sm(14), sm(13), A.add, ["sm13", "sm14"], "off0", n / 2.0, A.is_le)
            act(T.gj[:, 0:32], T.ft[:, :].indirect(T.off[:, 0:2]), AF.Identity, ["off0", "off1", "sc8"] + FT, ["gj", nx], scale=T.sc8[:, r:r + 1], accum_out=sm(16 + r))
            t, tk = sm(16 + r), nx
            job()
        for _ in jobs:
            pass
        tr, trk = (T.tr1, "tr1") if n == 512 else (T.tr2, "tr2")
        ts(T.gt[:, 0:q], ch[:, :], t, A.is_gt, ["ch", tk], "gt")
        ts(T.eq[:, 0:q], ch[:, :], t, A.is_equal, ["ch", tk], "eq")
        scan(T.ges[:, 1:q + 1], T.gt[:, 0:q], T.zero[:, 0:q], ["gt", "zero", "ges0"], "gs")
        scan(T.ges[:, 37:q + 37], T.eq[:, 0:q], T.zero[:, 0:q], ["eq", "zero", "ges0"], "es")
        ts(T.lt[:, 0:q], ch[:, :], t, A.is_lt, ["ch", tk], "lt", 1024.0, A.mult)
        ts(T.og[:, 0:2], T.ges[:, q:q + 37:36], cc(L33), A.add, ["gs", "es", "l33"], "og")
        act(T.gj[:, 0:16], T.ps[:, 528:1056].indirect(T.og[:, 0:1]), AF.Identity, ["og"] + PS, ["gj", "sm31"], scale=-1.0, bias=n / 32.0, accum_out=sm(31))
        act(T.gj[:, 32:64], T.ps[:, 0:528].indirect(T.og[:, 0:2]), AF.Identity, ["og"] + PS, ["gk", "sm32"], accum_out=sm(32))
        ts(T.ngt[:, 0:q], ch[:, :], t, A.is_le, ["ch", tk], "ngt")
        tt(T.es2[:, 0:q], T.ges[:, 36:q + 36], T.lt[:, 0:q], A.add, ["es", "ges0", "lt"], "es2")
        tt(T.trn[:, 0:q], T.ngt[:, 0:q], tr[:, :], A.mult, ["ngt", trk], "trn")
        ts(T.me[:, 0:q], T.es2[:, 0:q], sm(32), A.add, ["es2", "sm32", "sm31"], "me", sm(31), A.min)
        ts(T.y1[:, 0:q], T.es2[:, 0:q], sm(32), A.add, ["es2", "sm32", "sm31"], "y1", sm(31), A.is_ge)
        tt(T.vi[:, 0:q], T.ges[:, 0:q], T.me[:, 0:q], A.add, ["gs", "ges0", "me"], "vi")
        tt(T.mm[:, 0:q], T.y1[:, 0:q], T.trn[:, 0:q], A.mult, ["y1", "trn"], "mm")
        tt(T.dd[:, 0:q], T.mm[:, 0:q], T.vi[:, 0:q], A.max, ["mm", "vi"], "dd")
        so, R, rk, val, vk, Tr = (T.osc1, T.R1, "R1", T.val1, "val1", T.Tr1) if n == 512 else (T.osc2, T.R2, "R2", T.val2, "val2", T.Tr2)
        ts(so[:, :], T.dd[:, 0:q], cc(O16), A.add, ["dd", "o16"], "so")
        cp(R[:, :].indirect(so[:, :]), val[:, :], ["so", vk], rk)
        m = n // 2
        turn(Tr[:, 0:m], R[:, 0:m], [rk], rk + "a")
        turn(Tr[:, m:n], R[:, 16:m + 16], [rk], rk + "b")

    L1T, L2T = ["R1a", "R1b", "sel1"], ["R2a", "R2b", "sel2"]

    def pick(c, tr, sel, n, k, add, r, o, w):
        ts(T[o][:, c:c + 16], T[tr][:, 0:n].indirect(T[sel][:, 0:1]), k, A.mult, r, w, add, A.add)

    def gather(dst, h, t, src, rs, o, eng, w):
        a = (T[dst][:, 512 * h + t:512 * h + 512:4], src[:, :].indirect(T[o][:, 16 * t + 8 * h:16 * t + 8 * h + 8]))
        if eng == "a":
            act(*a, AF.Copy, rs, [w])
        else:
            cp(*a, rs, w)

    def relu(dst, h, b, p, eng, w):
        o, i = T[dst][:, 512 * h + b:512 * h + 512:4], T[p][:, 0:128]
        if eng == "a":
            act(o, i, AF.Relu, [p], [w], scale=0.03125)
        else:
            ts(o, i, 0.0, A.max, [p], w, 0.03125, A.mult)

    def four(n):
        return ["%s%d" % (n, t) for t in range(4)]

    search(512, "p0", "p1", (("p2", 256), ("p3", 256)), 64, T.ch1, jobs1())
    dma("s", T.tv[:, :], T.v[:, :], w=["tv"])
    dma("s", codes(T.qZ[:, :]), T.zc[:, :], w=["qZ"])
    dma("s", T.sZ[:, :], T.zs[:, :], w=["sZ"])
    dma("s", T.xf[:, :], T.x[:, :], w=["xf0"])
    for t in range(4):
        pick(16 * t, "Tr1", "sel1", 512, 4.0, 1024.0 + t, L1T, "o1", "o1_%d" % t)
    FA, FB, HA, HB = four("tfa"), four("tfb"), four("tha"), four("thb")
    for t in range(4):
        gather("tf", 0, t, T.tx, X + ["o1_%d" % t], "o1", "avav"[t], FA[t])
    for t in range(3):
        gather("tf", 1, t, T.tx, X + ["o1_%d" % t], "o1", "ava"[t], FB[t])
    quant("F", 0, 128, T.tf, FA, "qFa")
    gather("tf", 1, 3, T.tx, X + ["o1_3"], "o1", "v", FB[3])
    quant("F", 128, 128, T.tf, FB, "qFb")
    PA, PB = ["p2", "p3", "p4", "p5"], ["p6", "p7", "p0", "p1"]
    for b in range(4):
        mm(PA[b], 128, "W", 128 * b, "F", 0, ["qW", "sW", "qFa"])
    for b in range(4):
        mm(PB[b], 128, "W", 128 * b, "F", 128, ["qW", "sW", "qFb"])
    for b in range(4):
        relu("th", 0, b, PA[b], "avav"[b], HA[b])
    relu("th", 1, 0, PB[0], "a", HB[0])
    relu("th", 1, 1, PB[1], "v", HB[1])
    quant("H", 0, 128, T.th, HA, "qHa")
    relu("th", 1, 2, PB[2], "a", HB[2])
    relu("th", 1, 3, PB[3], "v", HB[3])
    quant("H", 128, 128, T.th, HB, "qHb")
    dma("s", T.txh[:, :], T.tf[:, :], r=FA + FB, w=["txh"])
    dma("g", T.txh[:, :], T.th[:, :], r=HA + HB, w=["txh"], accum_op=A.add)
    for p in ("p2", "p3"):
        mm(p, 256, "r2", 0, "H", 0, ["qHa", "qHb", "qr2", "sr2"])
    search(256, "p2", "p3", None, 0, T.ch2, jobs2())
    for t in range(4):
        pick(16 * t, "Tr2", "sel2", 256, 4.0, float(t), L2T, "o2", "o2_%d" % t)
    for t in range(4):
        gather("tg", 0, t, T.th, HA + HB + ["o2_%d" % t], "o2", "avav"[t], "tg%d" % t)
    quant("G", 0, 128, T.tg, four("tg"), "qG")

    far = [d for d in range(N) if d != rank and topo.die(T.cores[d]) != topo.die(core)]
    near = [d for d in range(N) if d != rank and topo.die(T.cores[d]) == topo.die(core)]
    masks = {}
    for lst, o in ((far, 0), (near, 1)):
        for j, d in enumerate(lst):
            e = topo.engines(core, T.cores[d])
            masks[d] = sum(1 << x for x in (e[4 * j + o], e[4 * j + o + 2]))
    order = sorted(masks, key=lambda d: (d - rank) % N)

    def swap(a, b, sem):
        own = slice(16 * rank, 16 * rank + 16)
        tok = "q" + a
        dma("s", codes(T["q" + b][:, own]), codes(T["q" + a][:, own]), r=[tok], w=[tok + "o"])
        dma("s", T["s" + b][:, own], T["s" + a][:, own], r=[tok], w=[tok + "p"])
        learn("g", wr[tok])
        for x in "qs":
            tr = []
            for d in order:
                rid, pid, _ = topo.addr(T.cores[d])
                src, dst = T[x + a][:, 16 * d:16 * d + 16], T[x + b][:, own]
                if x == "q":
                    src, dst = codes(src), codes(dst)
                tr.append(RemoteDMATransfer(dst_ids=[DstId(rid=rid, pnc=pid)], dma_engine_mask=masks[d], remote_sem=T.sem[sem], src=src, dst=dst))
            g.remote_dma_fused(tr, local_sem=T.sem.sent)
        total[sem] = 4 * (N - 1)
        wr[tok + "r"] = [("far", sem, total[sem], {})]
        total["sent"] = total.get("sent", 0) + 4 * (N - 1)
    swap("G", "L", "down")
    pick(64, "Tr1", "sel1", 512, 1.0, 256.0, L1T, "o1", "o1c")
    pick(64, "Tr2", "sel2", 256, 1.0, 0.0, L2T, "o2", "o2c")
    act(T.L1r[:, :], T.ir[:, :].indirect(T.o1[:, 64:80]), AF.Identity, ["ir", "o1c"], ["L1r"])
    act(T.olr[:, :], T.L1r[:, :].indirect(T.o2[:, 64:72]), AF.Identity, ["L1r", "o2c"], ["olr"])
    dma("s", T.ol[:, :], T.olr[0:128:16, :], r=["olr"], w=["ol"])
    act(T.gap3[:, :], T.olr[:, :].indirect(T.orep[:, 0:33]), AF.Identity, ["olr", "orep"], ["gap3"], bias=-256.0)
    ts(T.sel3[:, 1:2], T.sel3[:, 0:1], 256.0, A.add, ["sel3a"], "sel3b")
    for t, h in ((1, 0), (1, 1), (2, 0)):
        base(t, h)
    for b in range(4):
        mm(PA[b], 128, "Z", 128 * b, "L", 0, ["qZ", "sZ", "qGo", "qGp", "qGr"])
    for b in range(4):
        relu("tt", 0, b, PA[b], "avav"[b], "tt%d" % b)
    quant("T", 0, 128, T.tt, four("tt"), "qT")
    swap("T", "U", "up")
    turn(T.Tr3[:, 0:512], T.gap3[:, 0:512], ["gap3"], "Tr3a")
    turn(T.Tr3[:, 512:1024], T.gap3[:, 16:528], ["gap3"], "Tr3b")
    ts(T.o3[:, :], T.Tr3[:, :].indirect(T.sel3[:, 0:2]), 4.0, A.mult, ["Tr3a", "Tr3b", "sel3a", "sel3b", "l4"], "o3", cc(L4), A.add)
    act(T.txg[:, :], T.tx[:, :].indirect(T.o3[:, :]), AF.Copy, X + ["o3"], ["txg"])
    for t, h in ((2, 1), (3, 0), (3, 1)):
        base(t, h)
    for b in range(4):
        mm(PA[b], 128, "E", 128 * b, "U", 0, ["qE%d" % b, "qTo", "qTp", "qTr"])
    for b in range(4):
        tt(T.thn[:, b:512:4], T[PA[b]][:, 0:128], T.tg[:, b:512:4], A.add, [PA[b], "tg%d" % b], "thn%d" % b)
    for b in range(4):
        tt(T.txn[:, b:512:4], T.txg[:, b:512:4], T.thn[:, b:512:4], A.add, ["txg", "thn%d" % b], "txn%d" % b)
    cp(T.xf[:, :].indirect(T.o3[:, :]), T.txn[:, :], ["o3"] + four("txn"), "xf")
    for h in range(4):
        quant("N", 128 * h, 128, T.xf, ["xf"], "qN%d" % h)
        mm(PB[h], 128, "v", 0, "N", 128 * h, ["qvv", "qN%d" % h])
    for h in range(4):
        o, i = T.ysb[:, 128 * h:128 * h + 128], T[PB[h]][:, 0:128]
        if h % 2 == 0:
            act(o, i, AF.Copy, [PB[h]], ["y%d" % h])
        else:
            cp(o, i, [PB[h]], "y%d" % h)
    dma("s", T.oc[:, 0:1024], codes(T.qN[:, 0:256]), r=["qN0", "qN1"], w=["oc0"])
    dma("s", T.oc[:, 1024:2048], codes(T.qN[:, 256:512]), r=["qN2", "qN3"], w=["oc1"])
    for j in range(4):
        dma("s", T.osc[4 * j:4 * j + 4, :], T.sN[32 * j:32 * j + 4, :], r=["qN%d" % h for h in range(4)], w=["osc%d" % j])
    dma("a", T.y[:, 0:256], T.ysb[:, 0:256], r=["y0", "y1"], w=["yo0"])
    dma("s", T.y[:, 256:512], T.ysb[:, 256:512], r=["y2", "y3"], w=["yo1"])
    for s in sorted(total):
        if seen.get(s, 0) < total[s]:
            g.wait_ge(T.sem[s], total[s])
